import numpy as np
import ml_dtypes


def mxq(x, axis, fmt="e4m3"):
    dtype, down = {"e4m3": (ml_dtypes.float8_e4m3fn, 7), "e5m2": (ml_dtypes.float8_e5m2, 14)}[fmt]
    v = np.moveaxis(np.asarray(x, np.float32).astype(ml_dtypes.bfloat16).astype(np.float64), axis, -1)
    blocks = v.reshape(v.shape[:-1] + (-1, 32))
    amax = np.abs(blocks).max(-1, keepdims=True)
    byte = np.maximum(np.where(amax > 0, np.frexp(amax)[1] - 1 + 127, 0) - down, 1)
    scale = np.exp2(byte - 127.0)
    codes = (blocks / scale).astype(np.float32).astype(dtype).astype(np.float64)
    return np.moveaxis((codes * scale).reshape(v.shape), -1, axis)


WIDE = False


def mx_kscale(k):
    if not WIDE:
        return np.ones(k)
    levels = np.array([10, -10, 5, -5, 0])
    if k % 512:
        return np.exp2(np.random.permutation(np.resize(levels, k // 32))).repeat(32)
    a = np.empty((k // 512, 16))
    for p in range(k // 512):
        a[p, :8] = np.random.permutation(np.resize(levels, 8))
        for g in range(8):
            far = levels[np.abs(levels - a[p, g]) >= 10]
            a[p, g + 8] = far[np.random.randint(len(far))]
    return np.exp2(a.ravel()).repeat(32)


def f64(x):
    return np.asarray(x).astype(np.float64)


def striped(idx):
    return np.tile(idx.reshape(-1, 16).T, (8, 1)).astype(np.uint16)


def unstriped(offs):
    return offs[:16].T.reshape(-1).astype(np.int64)


E2M1 = np.array([0.0, 0.5, 1.0, 1.5, 2.0, 3.0, 4.0, 6.0, -0.0, -0.5, -1.0, -1.5, -2.0, -3.0, -4.0, -6.0])


def pack_weight(w, fmt):
    k, n = w.shape
    w = f64(np.asarray(w, np.float32).astype(ml_dtypes.bfloat16)).reshape(k // 32, 32, n)
    amax = np.abs(w).max(1)
    if fmt == "e4m3":
        byte = np.frexp(amax)[1] - 1 + 127 - 7
    else:
        mant, ex = np.frexp(amax / 6.0)
        byte = np.where(mant > 0.5, ex, ex - 1) + 127
    byte = np.clip(np.where(amax > 0, byte, 1), 1, 254)
    scaled = (w * np.exp2(127.0 - byte)[:, None, :]).reshape(k, n).astype(np.float32)
    by_word = np.ascontiguousarray(scaled.reshape(k // 512, 128, 4, n).transpose(0, 1, 3, 2))
    if fmt == "e4m3":
        words = by_word.astype(ml_dtypes.float8_e4m3fn).view(np.uint8)
    else:
        c = by_word.astype(ml_dtypes.float4_e2m1fn).view(np.uint8) & 0xF
        words = (c[..., 0::2] | (c[..., 1::2] << 4)).reshape(k // 512, 128, 2 * n)
    return np.ascontiguousarray(words), np.ascontiguousarray(byte.astype(np.uint8).reshape(k // 512, 16, n))


def unpack_weight(words, scales, fmt):
    g, _, n = scales.shape
    words = np.ascontiguousarray(words).reshape(g, 128, n, -1)
    if fmt == "e4m3":
        vals = words.view(ml_dtypes.float8_e4m3fn).astype(np.float64)
    else:
        nib = np.empty((g, 128, n, 4), np.uint8)
        nib[..., 0::2] = words & 0xF
        nib[..., 1::2] = words >> 4
        vals = E2M1[nib]
    vals = vals * np.repeat(np.exp2(scales.astype(np.float64) - 127.0), 8, axis=1)[..., None]
    return vals.transpose(0, 1, 3, 2).reshape(g * 512, n)


def gelu(v):
    return 0.5 * v * (1.0 + np.tanh(np.sqrt(2.0 / np.pi) * (v + 0.044715 * v**3)))


K, H, T, S, T2, P = 512, 1024, 4096, 1024, 2048, 1024

def setup_inputs():
    n = np.random.standard_normal
    s = mx_kscale(K)[:, None]
    u = mx_kscale(H)[:, None]
    tab_words, tab_scales = pack_weight(n((K, T)) * s, "e4m3")
    w4_words, w4_scales = pack_weight(n((K, H)) / np.sqrt(K) / s * u.T, "e2m1")
    wa = (n((K, H)) / np.sqrt(K) / s * u.T).astype(np.float32)
    wd = (n((H, H)) / np.sqrt(H) / u * u.T).astype(np.float32)
    dv = ((n(H) - 0.8) * u[:, 0]).astype(np.float32)
    amb = (0.8 * n((H, P)) * u).astype(np.float32)
    page0 = (n((H, T2)) * u).astype(np.float32)
    wgs = np.exp(0.3 * n((128, S))).astype(np.float32)
    wgo = np.exp(0.3 * n((128, P))).astype(np.float32)
    offs = striped(np.random.permutation(T)[:S])
    offs2 = striped(np.random.permutation(T2)[:S])
    offs3 = striped(np.random.permutation(T2)[:P])
    offs4 = striped(np.random.permutation(T2)[:P])
    return {"tab_words": tab_words, "tab_scales": tab_scales, "w4_words": w4_words, "w4_scales": w4_scales,
            "wa": wa, "wd": wd, "dv": dv, "amb": amb, "page0": page0, "wgs": wgs, "wgo": wgo,
            "offs": offs, "offs2": offs2, "offs3": offs3, "offs4": offs4}

def reference(tab_words, tab_scales, w4_words, w4_scales, wa, wd, dv, amb, page0, wgs, wgo,
              offs, offs2, offs3, offs4):
    v = unpack_weight(tab_words, tab_scales, "e4m3")[:, unstriped(offs)]
    ha = mxq(f64(wa), 0, "e4m3").T @ v
    hb = unpack_weight(w4_words, w4_scales, "e2m1").T @ v
    h = ha + np.abs(hb)
    page = f64(page0).copy()
    page[:, unstriped(offs2)] = np.tile(f64(wgs), (H // 128, 1)) * h
    x = page[:, unstriped(offs3)]
    z = np.abs(x) + f64(dv)[:, None]
    y = (mxq(f64(wd), 0, "e4m3").T @ mxq(z, 0, "e4m3")) + f64(amb)
    page[:, unstriped(offs4)] = np.tile(f64(wgo), (H // 128, 1)) * y
    return page

@@ -1,0 +1,270 @@
+from contextlib import ExitStack
+
+import concourse.mybir as mybir
+from concourse.masks import make_identity
+
+K, H, T, S, T2 = 512, 1024, 4096, 1024, 2048
+FLOPS = 2 * (2 * K * H * S + H * H * S)
+
+F32 = mybir.dt.float32
+BF16 = mybir.dt.bfloat16
+I32 = mybir.dt.int32
+U32 = mybir.dt.uint32
+U16 = mybir.dt.uint16
+U8 = mybir.dt.uint8
+FP8X4 = mybir.dt.float8_e4m3fn_x4
+FP4X4 = mybir.dt.float4_e2m1fn_x4
+ABS = mybir.ActivationFunctionType.Abs
+IDENTITY = mybir.ActivationFunctionType.Identity
+MULT = mybir.AluOpType.mult
+
+P = 128
+PACK = 4
+PASS = P * PACK
+HALF = 512
+SLICES = H // P
+LIST_COLS = HALF // 16
+
+
+def tile_list_reefer_fault_board_kernel(
+    tc, tab_words, tab_scales, w4_words, w4_scales, wa, wd, dv, amb, page0, wgs, wgo, offs, offs2, offs3, offs4, out
+):
+    nc = tc.nc
+    with ExitStack() as ctx:
+        keep = ctx.enter_context(tc.tile_pool(name="keep", bufs=1))
+        ring = ctx.enter_context(tc.tile_pool(name="ring", bufs=2))
+        psum = ctx.enter_context(tc.psum_pool(name="psum", bufs=3))
+
+        def load_list(source, name):
+            tile = keep.tile([P, S // 16], U16, name=name)
+            nc.sync.dma_start(tile[:], source)
+            return tile
+
+        def list_half(tile, half):
+            return tile[:, half * LIST_COLS : (half + 1) * LIST_COLS]
+
+        def load_scale_rows(tile, source):
+            for q in range(4):
+                rows = source[0, 4 * q : 4 * q + 4, :].bitcast(I32)
+                nc.sync.dma_start(tile[32 * q : 32 * (q + 1), :].bitcast(I32), rows.partition_broadcast(8))
+
+        def slice_rows(matrix, s):
+            b, t = divmod(s, PACK)
+            return matrix[PASS * b : PASS * (b + 1), :].rearrange("(p t) c -> t p c", t=PACK)[t]
+
+        def load_weight_block(matrix, a, b):
+            raw = ring.tile([P, PACK, PASS], F32, name="raw", tag="raw", align_bytes=64)
+            rows = matrix[PASS * a : PASS * (a + 1), PASS * b : PASS * (b + 1)]
+            nc.sync.dma_start(raw[:], rows.rearrange("(p i) c -> p i c", i=PACK))
+            return raw
+
+        def quantize_weight_block(raw, name):
+            woven = ring.tile([P, PACK * PASS], BF16, name="woven", tag="bf", bufs=3, align_bytes=64)
+            nc.scalar.copy(
+                woven[:].rearrange("p (t m i) -> p m t i", t=PACK, i=PACK),
+                raw[:].rearrange("p i (m t) -> p m t i", t=PACK),
+            )
+            codes = keep.tile([P, PASS], U32, name=name + "_codes", align_bytes=64)
+            scales = keep.tile([P, PASS], U8, name=name + "_scales", align_bytes=64)
+            nc.vector.quantize_mx(codes[:].bitcast(FP8X4), scales[:], woven[:])
+            return codes, scales
+
+        def load_row_weights(tile, source, t_from, t_to):
+            rows = source.rearrange("(q t) c -> q t c", t=PACK)[:, t_from:t_to, :]
+            for q in range(4):
+                nc.sync.dma_start(tile[32 * q : 32 * (q + 1), t_from:t_to, :], rows)
+
+        pages = [keep.tile([P, T2], F32, name="page%d" % s) for s in range(SLICES)]
+
+        def load_page(s):
+            nc.sync.dma_start(pages[s][:], slice_rows(page0, s))
+
+        table_scales = keep.tile([P, T], U8, name="table_scales")
+        w4_raw_scales = ring.tile([P, H], U8, name="w4_raw_scales", tag="x", bufs=4)
+        identity = keep.tile([P, P], F32, name="identity")
+        make_identity(nc, identity[:])
+
+        list1 = load_list(offs, "list1")
+        load_scale_rows(w4_raw_scales, w4_scales)
+        w4_raw = ring.tile([P, 2 * H], U8, name="w4_raw", tag="x", bufs=4)
+        nc.sync.dma_start(w4_raw[:].bitcast(I32), w4_words[0].bitcast(I32))
+        wa_raw0 = load_weight_block(wa, 0, 0)
+        table_words = keep.tile([P, T], U32, name="table_words")
+        nc.sync.dma_start(table_words[:].bitcast(I32), tab_words[0].rearrange("p c i -> p (c i)").bitcast(I32))
+        load_scale_rows(table_scales, tab_scales)
+        load_page(0)
+        list2 = load_list(offs2, "list2")
+        wgs_rows = keep.tile([P, PACK, S], F32, name="wgs_rows")
+        load_row_weights(wgs_rows, wgs, 0, 1)
+        list3 = load_list(offs3, "list3")
+        load_page(1)
+        load_row_weights(wgs_rows, wgs, 1, PACK)
+        wa_raw1 = load_weight_block(wa, 0, 1)
+        dv_rows = keep.tile([P, 2, PACK], F32, name="dv_rows")
+        nc.sync.dma_start(dv_rows[:], dv.rearrange("(b p t) -> p b t", b=2, t=PACK))
+
+        w4_codes = keep.tile([P, 2 * H], U8, name="w4_codes", align_bytes=64)
+        w4_plane = keep.tile([P, H], U8, name="w4_plane", align_bytes=64)
+        nc.vector.tensor_copy(
+            w4_codes[:].bitcast(U16).rearrange("p (b t m) -> p b m t", b=2, t=PACK),
+            w4_raw[:].bitcast(U16).rearrange("p (b m t) -> p b m t", b=2, t=PACK),
+        )
+        nc.vector.tensor_copy(
+            w4_plane[:].rearrange("p (b t m) -> p b m t", b=2, t=PACK),
+            w4_raw_scales[:].rearrange("p (b m t) -> p b m t", b=2, t=PACK),
+        )
+        wa_q = [quantize_weight_block(wa_raw0, "wa0")]
+
+        picked = []
+        for half in range(2):
+            words = keep.tile([P, HALF], U32, name="picked_words%d" % half, align_bytes=64)
+            plane = keep.tile([P, HALF], U8, name="picked_scales%d" % half, align_bytes=64)
+            nc.vector.tensor_copy(words[:], table_words[:].indirect(list_half(list1, half)))
+            nc.vector.tensor_copy(plane[:], table_scales[:].indirect(list_half(list1, half)))
+            picked.append((words, plane))
+
+        def add_transposed(first, second, result):
+            bank = psum.tile([P, HALF], F32, name="sum_bank", bufs=2)
+            for j in range(HALF // P):
+                cols = slice(j * P, (j + 1) * P)
+                nc.tensor.matmul(bank[:, cols], first[:, cols], identity[:], start=True, stop=False, is_transpose=True)
+                nc.tensor.matmul(bank[:, cols], second[:, cols], identity[:], start=False, stop=True, is_transpose=True)
+            nc.scalar.copy(result, bank[:])
+
+        def features(s, half, result):
+            b, t = divmod(s, PACK)
+            words, plane = picked[half]
+            wa_codes, wa_scales = wa_q[b]
+            own = slice(t * P, (t + 1) * P)
+            bank_a = psum.tile([P, HALF], F32, name="bank_a")
+            bank_b = psum.tile([P, HALF], F32, name="bank_b")
+            for j in range(HALF // P):
+                cols = slice(j * P, (j + 1) * P)
+                nc.tensor.matmul_mx(
+                    bank_a[:, cols], words[:, cols].bitcast(FP8X4), plane[:, cols],
+                    wa_codes[:, own].bitcast(FP8X4), wa_scales[:, own], start=True, stop=True,
+                )
+                nc.tensor.matmul_mx(
+                    bank_b[:, cols], words[:, cols].bitcast(FP8X4), plane[:, cols],
+                    w4_codes[:, 2 * s * P : 2 * (s + 1) * P].bitcast(FP4X4), w4_plane[:, s * P : (s + 1) * P],
+                    start=True, stop=True,
+                )
+            term_a = ring.tile([P, HALF], F32, name="term_a", bufs=3)
+            term_b = ring.tile([P, HALF], F32, name="term_b", bufs=3)
+            nc.scalar.copy(term_a[:], bank_a[:])
+            nc.scalar.activation(term_b[:], bank_b[:], ABS)
+            add_transposed(term_a, term_b, result)
+
+        h_tiles = {}
+
+        def make_h(s):
+            h_tiles[s] = ring.tile([P, S], F32, name="h", bufs=3)
+            for half in range(2):
+                features(s, half, h_tiles[s][:, half * HALF : (half + 1) * HALF])
+
+        def put_h(s):
+            t = s % PACK
+            if s == 0:
+                for half in range(2):
+                    cols = slice(half * HALF, (half + 1) * HALF)
+                    nc.vector.tensor_tensor(
+                        pages[s][:].indirect(list_half(list2, half)), h_tiles[s][:, cols], wgs_rows[:, t, cols], MULT
+                    )
+            else:
+                nc.vector.tensor_tensor(pages[s][:].indirect(list2[:]), h_tiles[s][:], wgs_rows[:, t, :], MULT)
+
+        def fetch(s, half, x):
+            nc.vector.tensor_copy(x, pages[s][:].indirect(list_half(list3, half)))
+
+        z_planes = {}
+
+        def make_z(s, half, x, woven):
+            b, t = divmod(s, PACK)
+            if t == 0:
+                z_planes[half] = ring.tile([P, PACK, HALF], BF16, name="z_planes", tag="bf", bufs=3, align_bytes=64)
+            planes = z_planes[half]
+            nc.scalar.activation(x, x, ABS)
+            nc.scalar.activation(planes[:, t, :], x, IDENTITY, bias=dv_rows[:, b, t : t + 1])
+            if t == PACK - 1:
+                target = woven[:, b * PACK * HALF : (b + 1) * PACK * HALF]
+                nc.scalar.copy(
+                    target.rearrange("p (c i t) -> p c t i", i=4, t=PACK),
+                    planes[:].rearrange("p t (c i) -> p c t i", i=4),
+                )
+
+        def quantize_z(half, woven):
+            codes = keep.tile([P, 2 * HALF], U32, name="z_codes%d" % half, align_bytes=64)
+            scales = keep.tile([P, 2 * HALF], U8, name="z_scales%d" % half, align_bytes=64)
+            nc.vector.quantize_mx(codes[:].bitcast(FP8X4), scales[:], woven)
+            return codes, scales
+
+        z_store = keep.tile([P, PACK * HALF], F32, name="z_store", align_bytes=64)
+        woven0 = z_store[:].bitcast(BF16)
+        wd_q = {}
+        wgo_rows = keep.tile([P, PACK, S], F32, name="wgo_rows")
+        make_h(0)
+        make_h(1)
+        wa_q.append(quantize_weight_block(wa_raw1, "wa1"))
+        x_first = {}
+        for s in range(SLICES):
+            if s + 2 < SLICES:
+                load_page(s + 2)
+                make_h(s + 2)
+            if s < 4:
+                a, b = divmod(s, 2)
+                wd_q[(a, b)] = quantize_weight_block(load_weight_block(wd, a, b), "wd%d" % s)
+            put_h(s)
+            x_first[s] = ring.tile([P, HALF], F32, name="x", tag="x", bufs=4)
+            fetch(s, 0, x_first[s][:])
+            if s >= 1:
+                make_z(s - 1, 0, x_first[s - 1][:], woven0)
+            if s == 4:
+                list4 = load_list(offs4, "list4")
+                load_row_weights(wgo_rows, wgo, 0, PACK)
+        make_z(SLICES - 1, 0, x_first[SLICES - 1][:], woven0)
+
+        last_h = h_tiles[SLICES - 1]
+        x_second = [wgs_rows[:, PACK - 1, 0:HALF], wgs_rows[:, PACK - 1, HALF:S], last_h[:, 0:HALF], last_h[:, HALF:S]]
+        x_second = x_second + [z_store[:, u * HALF : (u + 1) * HALF] for u in range(PACK)]
+        for s in range(PACK):
+            fetch(s, 1, x_second[s])
+        z_q = [quantize_z(0, woven0)]
+        for s in range(PACK, SLICES):
+            fetch(s, 1, x_second[s])
+
+        def update(s, half):
+            b, t = divmod(s, PACK)
+            cols_half = slice(half * HALF, (half + 1) * HALF)
+            ambient = ring.tile([P, HALF], F32, name="ambient", bufs=4)
+            nc.sync.dma_start(ambient[:], slice_rows(amb, s)[:, cols_half])
+            bank_b = psum.tile([P, HALF], F32, name="bank_b")
+            for j in range(HALF // P):
+                cols = slice(j * P, (j + 1) * P)
+                nc.tensor.transpose(bank_b[:, cols], ambient[:, cols], identity[:])
+            term_b = ring.tile([P, HALF], F32, name="term_b", bufs=3)
+            nc.scalar.copy(term_b[:], bank_b[:])
+            z_codes, z_scales = z_q[half]
+            own = slice(t * P, (t + 1) * P)
+            bank_a = psum.tile([P, HALF], F32, name="bank_a")
+            for j in range(HALF // P):
+                for a in range(2):
+                    cols = slice(a * HALF + j * P, a * HALF + (j + 1) * P)
+                    wd_codes, wd_scales = wd_q[(a, b)]
+                    nc.tensor.matmul_mx(
+                        bank_a[:, j * P : (j + 1) * P], z_codes[:, cols].bitcast(FP8X4), z_scales[:, cols],
+                        wd_codes[:, own].bitcast(FP8X4), wd_scales[:, own], start=(a == 0), stop=(a == 1),
+                    )
+            term_a = ring.tile([P, HALF], F32, name="term_a", bufs=3)
+            nc.scalar.copy(term_a[:], bank_a[:])
+            y = ring.tile([P, HALF], F32, name="y", tag="x", bufs=4)
+            add_transposed(term_a, term_b, y[:])
+            nc.vector.tensor_tensor(pages[s][:].indirect(list_half(list4, half)), y[:], wgo_rows[:, t, cols_half], MULT)
+
+        second_store = ring.tile([P, 2 * PACK * HALF], BF16, name="second_store", tag="raw", align_bytes=64)
+        for s in range(SLICES):
+            update(s, 0)
+            make_z(s, 1, x_second[s], second_store[:])
+        z_q.append(quantize_z(1, second_store[:]))
+        for s in range(SLICES):
+            update(s, 1)
+            nc.sync.dma_start(slice_rows(out, s), pages[s][:])

@@ -17,6 +17,7 @@ FP4X4 = mybir.dt.float4_e2m1fn_x4
 ABS = mybir.ActivationFunctionType.Abs
 IDENTITY = mybir.ActivationFunctionType.Identity
 MULT = mybir.AluOpType.mult
+ADD = mybir.AluOpType.add
 
 P = 128
 PACK = 4
@@ -24,6 +25,19 @@ PASS = P * PACK
 HALF = 512
 SLICES = H // P
 LIST_COLS = HALF // 16
+DIRECT1 = [(0, 0), (0, 1)]
+DIRECT2 = [(0, 0), (2, 0), (0, 1)]
+Z_AFTER = [2, 1, 2, 1, 1, 1, 0, 0]
+
+
+def take(turns):
+    count = turns["taken"]
+    turns["taken"] = count + 1
+    return turns["tiles"][count % len(turns["tiles"])]
+
+
+def cycle(tiles):
+    return {"tiles": tiles, "taken": 0}
 
 
 def tile_list_reefer_fault_board_kernel(
@@ -32,8 +46,21 @@ def tile_list_reefer_fault_board_kernel(
     nc = tc.nc
     with ExitStack() as ctx:
         keep = ctx.enter_context(tc.tile_pool(name="keep", bufs=1))
-        ring = ctx.enter_context(tc.tile_pool(name="ring", bufs=2))
-        psum = ctx.enter_context(tc.psum_pool(name="psum", bufs=3))
+        psum = ctx.enter_context(tc.psum_pool(name="psum", bufs=1))
+
+        def rotation(pool, name, count, shape, dtype):
+            return cycle([pool.tile(shape, dtype, name="%s%d" % (name, n), align_bytes=64) for n in range(count)])
+
+        raw_tiles = rotation(keep, "raw", 2, [P, PACK, PASS], F32)
+        woven_tiles = rotation(keep, "woven", 2, [P, PACK * PASS], BF16)
+        a_terms = rotation(keep, "term_a", 3, [P, HALF], F32)
+        b_terms = rotation(keep, "term_b", 5, [P, HALF], F32)
+        h_ring = rotation(keep, "h", 3, [P, S], F32)
+        x_ring = rotation(keep, "x", 4, [P, HALF], F32)
+        ambient_tiles = rotation(keep, "ambient", 4, [P, HALF], F32)
+        a_banks = cycle([psum.tile([P, HALF], F32, name="bank_a%d" % n) for n in range(3)])
+        b_banks = cycle([psum.tile([P, HALF], F32, name="bank_b%d" % n) for n in range(3)])
+        sum_banks = cycle([psum.tile([P, HALF], F32, name="sum_bank%d" % n) for n in range(2)])
 
         def load_list(source, name):
             tile = keep.tile([P, S // 16], U16, name=name)
@@ -43,36 +70,40 @@ def tile_list_reefer_fault_board_kernel(
         def list_half(tile, half):
             return tile[:, half * LIST_COLS : (half + 1) * LIST_COLS]
 
+        def half_cols(half):
+            return slice(half * HALF, (half + 1) * HALF)
+
         def load_scale_rows(tile, source):
             for q in range(4):
                 rows = source[0, 4 * q : 4 * q + 4, :].bitcast(I32)
-                nc.sync.dma_start(tile[32 * q : 32 * (q + 1), :].bitcast(I32), rows.partition_broadcast(8))
+                nc.gpsimd.dma_start(tile[32 * q : 32 * q + 4, :].bitcast(I32), rows)
 
         def slice_rows(matrix, s):
             b, t = divmod(s, PACK)
             return matrix[PASS * b : PASS * (b + 1), :].rearrange("(p t) c -> t p c", t=PACK)[t]
 
         def load_weight_block(matrix, a, b):
-            raw = ring.tile([P, PACK, PASS], F32, name="raw", tag="raw", align_bytes=64)
+            raw = take(raw_tiles)
             rows = matrix[PASS * a : PASS * (a + 1), PASS * b : PASS * (b + 1)]
             nc.sync.dma_start(raw[:], rows.rearrange("(p i) c -> p i c", i=PACK))
             return raw
 
-        def quantize_weight_block(raw, name):
-            woven = ring.tile([P, PACK * PASS], BF16, name="woven", tag="bf", bufs=3, align_bytes=64)
+        def weave_weight_block(raw):
+            woven = take(woven_tiles)
             nc.scalar.copy(
                 woven[:].rearrange("p (t m i) -> p m t i", t=PACK, i=PACK),
-                raw[:].rearrange("p i (m t) -> p m t i", t=PACK),
+                raw.rearrange("p i (m t) -> p m t i", t=PACK),
             )
-            codes = keep.tile([P, PASS], U32, name=name + "_codes", align_bytes=64)
+            return woven
+
+        def quantize_weight_block(woven, codes, name):
             scales = keep.tile([P, PASS], U8, name=name + "_scales", align_bytes=64)
-            nc.vector.quantize_mx(codes[:].bitcast(FP8X4), scales[:], woven[:])
+            nc.vector.quantize_mx(codes.bitcast(FP8X4), scales[:], woven[:])
             return codes, scales
 
-        def load_row_weights(tile, source, t_from, t_to):
-            rows = source.rearrange("(q t) c -> q t c", t=PACK)[:, t_from:t_to, :]
+        def load_row_weights(tile, rows):
             for q in range(4):
-                nc.sync.dma_start(tile[32 * q : 32 * (q + 1), t_from:t_to, :], rows)
+                nc.sync.dma_start(tile[32 * q : 32 * (q + 1)], rows)
 
         pages = [keep.tile([P, T2], F32, name="page%d" % s) for s in range(SLICES)]
 
@@ -80,111 +111,147 @@ def tile_list_reefer_fault_board_kernel(
             nc.sync.dma_start(pages[s][:], slice_rows(page0, s))
 
         table_scales = keep.tile([P, T], U8, name="table_scales")
-        w4_raw_scales = ring.tile([P, H], U8, name="w4_raw_scales", tag="x", bufs=4)
+        nc.vector.memset(table_scales[:].bitcast(I32), 0)
+        load_scale_rows(table_scales, tab_scales)
         identity = keep.tile([P, P], F32, name="identity")
         make_identity(nc, identity[:])
 
         list1 = load_list(offs, "list1")
-        load_scale_rows(w4_raw_scales, w4_scales)
-        w4_raw = ring.tile([P, 2 * H], U8, name="w4_raw", tag="x", bufs=4)
+        w4_raw_scales = keep.tile([P, H], U8, name="w4_raw_scales")
+        for q in range(4):
+            rows = w4_scales[0, 4 * q : 4 * q + 4, :].bitcast(I32)
+            nc.sync.dma_start(w4_raw_scales[32 * q : 32 * (q + 1), :].bitcast(I32), rows.partition_broadcast(8))
+        w4_raw = keep.tile([P, 2 * H], U8, name="w4_raw")
         nc.sync.dma_start(w4_raw[:].bitcast(I32), w4_words[0].bitcast(I32))
         wa_raw0 = load_weight_block(wa, 0, 0)
-        table_words = keep.tile([P, T], U32, name="table_words")
+        table_words = keep.tile([P, T], U32, name="table_words", tag="wide")
         nc.sync.dma_start(table_words[:].bitcast(I32), tab_words[0].rearrange("p c i -> p (c i)").bitcast(I32))
-        load_scale_rows(table_scales, tab_scales)
         load_page(0)
         list2 = load_list(offs2, "list2")
-        wgs_rows = keep.tile([P, PACK, S], F32, name="wgs_rows")
-        load_row_weights(wgs_rows, wgs, 0, 1)
+        wgs_rows = [keep.tile([P, S], F32, name="wgs_rows%d" % t, align_bytes=64) for t in range(PACK)]
+        wgs_dealt = wgs.rearrange("(q t) c -> t q c", t=PACK)
+        for half in range(2):
+            load_row_weights(wgs_rows[0][:, half_cols(half)], wgs_dealt[0][:, half_cols(half)])
         list3 = load_list(offs3, "list3")
-        load_page(1)
-        load_row_weights(wgs_rows, wgs, 1, PACK)
-        wa_raw1 = load_weight_block(wa, 0, 1)
-        dv_rows = keep.tile([P, 2, PACK], F32, name="dv_rows")
-        nc.sync.dma_start(dv_rows[:], dv.rearrange("(b p t) -> p b t", b=2, t=PACK))
+        for s in range(1, PACK):
+            load_page(s)
+            load_row_weights(wgs_rows[s][:], wgs_dealt[s])
+            if s == 1:
+                wa_raw1 = load_weight_block(wa, 0, 1)
+                dv_rows = keep.tile([P, 2, PACK], F32, name="dv_rows")
+                nc.sync.dma_start(dv_rows[:], dv.rearrange("(b p t) -> p b t", b=2, t=PACK))
+        wd_wide = keep.tile([P, PACK, H], F32, name="wd_wide", tag="wide")
+        nc.sync.dma_start(wd_wide[:], wd[0:PASS, :].rearrange("(p i) c -> p i c", i=PACK))
+        load_page(4)
+        wd_raw = {(0, 0): wd_wide[:, :, 0:PASS], (0, 1): wd_wide[:, :, PASS:H]}
 
         w4_codes = keep.tile([P, 2 * H], U8, name="w4_codes", align_bytes=64)
         w4_plane = keep.tile([P, H], U8, name="w4_plane", align_bytes=64)
         nc.vector.tensor_copy(
-            w4_codes[:].bitcast(U16).rearrange("p (b t m) -> p b m t", b=2, t=PACK),
-            w4_raw[:].bitcast(U16).rearrange("p (b m t) -> p b m t", b=2, t=PACK),
-        )
-        nc.vector.tensor_copy(
             w4_plane[:].rearrange("p (b t m) -> p b m t", b=2, t=PACK),
             w4_raw_scales[:].rearrange("p (b m t) -> p b m t", b=2, t=PACK),
         )
-        wa_q = [quantize_weight_block(wa_raw0, "wa0")]
+        nc.vector.tensor_copy(
+            w4_codes[:].bitcast(U16).rearrange("p (b t m) -> p b m t", b=2, t=PACK),
+            w4_raw[:].bitcast(U16).rearrange("p (b m t) -> p b m t", b=2, t=PACK),
+        )
+        wa0_codes = keep.tile([P, PASS], U32, name="wa0_codes", align_bytes=64)
+        wa_q = [quantize_weight_block(weave_weight_block(wa_raw0[:]), wa0_codes[:], "wa0")]
 
         picked = []
         for half in range(2):
             words = keep.tile([P, HALF], U32, name="picked_words%d" % half, align_bytes=64)
             plane = keep.tile([P, HALF], U8, name="picked_scales%d" % half, align_bytes=64)
-            nc.vector.tensor_copy(words[:], table_words[:].indirect(list_half(list1, half)))
             nc.vector.tensor_copy(plane[:], table_scales[:].indirect(list_half(list1, half)))
+            nc.vector.tensor_copy(words[:], table_words[:].indirect(list_half(list1, half)))
             picked.append((words, plane))
 
+        def product(bank, moving_side, passes):
+            if moving_side == "tokens":
+                for a, (codes, scales, w_codes, w_scales) in enumerate(passes):
+                    nc.tensor.matmul_mx(
+                        bank[:], w_codes, w_scales, codes.bitcast(FP8X4), scales,
+                        start=(a == 0), stop=(a == len(passes) - 1),
+                    )
+                return
+            for j in range(HALF // P):
+                cols = slice(j * P, (j + 1) * P)
+                for a, (codes, scales, w_codes, w_scales) in enumerate(passes):
+                    nc.tensor.matmul_mx(
+                        bank[:, cols], codes[:, cols].bitcast(FP8X4), scales[:, cols], w_codes, w_scales,
+                        start=(a == 0), stop=(a == len(passes) - 1),
+                    )
+
         def add_transposed(first, second, result):
-            bank = psum.tile([P, HALF], F32, name="sum_bank", bufs=2)
+            bank = take(sum_banks)
             for j in range(HALF // P):
                 cols = slice(j * P, (j + 1) * P)
                 nc.tensor.matmul(bank[:, cols], first[:, cols], identity[:], start=True, stop=False, is_transpose=True)
                 nc.tensor.matmul(bank[:, cols], second[:, cols], identity[:], start=False, stop=True, is_transpose=True)
             nc.scalar.copy(result, bank[:])
 
-        def features(s, half, result):
+        def to_sbuf(bank, terms):
+            term = take(terms)
+            nc.scalar.copy(term[:], bank[:])
+            return term
+
+        def feature_terms(s, half):
             b, t = divmod(s, PACK)
             words, plane = picked[half]
             wa_codes, wa_scales = wa_q[b]
             own = slice(t * P, (t + 1) * P)
-            bank_a = psum.tile([P, HALF], F32, name="bank_a")
-            bank_b = psum.tile([P, HALF], F32, name="bank_b")
-            for j in range(HALF // P):
-                cols = slice(j * P, (j + 1) * P)
-                nc.tensor.matmul_mx(
-                    bank_a[:, cols], words[:, cols].bitcast(FP8X4), plane[:, cols],
-                    wa_codes[:, own].bitcast(FP8X4), wa_scales[:, own], start=True, stop=True,
-                )
-                nc.tensor.matmul_mx(
-                    bank_b[:, cols], words[:, cols].bitcast(FP8X4), plane[:, cols],
-                    w4_codes[:, 2 * s * P : 2 * (s + 1) * P].bitcast(FP4X4), w4_plane[:, s * P : (s + 1) * P],
-                    start=True, stop=True,
-                )
-            term_a = ring.tile([P, HALF], F32, name="term_a", bufs=3)
-            term_b = ring.tile([P, HALF], F32, name="term_b", bufs=3)
-            nc.scalar.copy(term_a[:], bank_a[:])
+            direct = (s, half) in DIRECT1
+            side = "tokens" if direct else "weights"
+            bank_a = take(a_banks)
+            bank_b = take(b_banks)
+            w4_own = w4_codes[:, 2 * s * P : 2 * (s + 1) * P].bitcast(FP4X4)
+            product(bank_b, side, [(words[:], plane[:], w4_own, w4_plane[:, s * P : (s + 1) * P])])
+            product(bank_a, side, [(words[:], plane[:], wa_codes[:, own].bitcast(FP8X4), wa_scales[:, own])])
+            term_b = take(b_terms)
             nc.scalar.activation(term_b[:], bank_b[:], ABS)
-            add_transposed(term_a, term_b, result)
+            return direct, (bank_a if direct else to_sbuf(bank_a, a_terms)), term_b
+
+        def add_terms(terms, result):
+            direct, term_a, term_b = terms
+            if direct:
+                nc.vector.tensor_tensor(result, term_a[:], term_b[:], ADD)
+            else:
+                add_transposed(term_a, term_b, result)
 
         h_tiles = {}
+        h_single = keep.tile([P, S], F32, name="h_single", align_bytes=64)
+        h_terms = {}
 
-        def make_h(s):
-            h_tiles[s] = ring.tile([P, S], F32, name="h", bufs=3)
-            for half in range(2):
-                features(s, half, h_tiles[s][:, half * HALF : (half + 1) * HALF])
+        def h_step(u):
+            if u + 1 < 2 * SLICES:
+                h_terms[u + 1] = feature_terms(*divmod(u + 1, 2))
+            if 0 <= u < 2 * SLICES:
+                s, half = divmod(u, 2)
+                if half == 0:
+                    h_tiles[s] = h_single if s == 1 else take(h_ring)
+                add_terms(h_terms[u], h_tiles[s][:, half_cols(half)])
 
         def put_h(s):
             t = s % PACK
             if s == 0:
                 for half in range(2):
-                    cols = slice(half * HALF, (half + 1) * HALF)
+                    cols = half_cols(half)
                     nc.vector.tensor_tensor(
-                        pages[s][:].indirect(list_half(list2, half)), h_tiles[s][:, cols], wgs_rows[:, t, cols], MULT
+                        pages[s][:].indirect(list_half(list2, half)), h_tiles[s][:, cols], wgs_rows[t][:, cols], MULT
                     )
             else:
-                nc.vector.tensor_tensor(pages[s][:].indirect(list2[:]), h_tiles[s][:], wgs_rows[:, t, :], MULT)
+                nc.vector.tensor_tensor(pages[s][:].indirect(list2[:]), h_tiles[s][:], wgs_rows[t][:], MULT)
 
         def fetch(s, half, x):
             nc.vector.tensor_copy(x, pages[s][:].indirect(list_half(list3, half)))
 
-        z_planes = {}
+        planes = keep.tile([P, PACK, HALF], BF16, name="z_planes")
 
         def make_z(s, half, x, woven):
             b, t = divmod(s, PACK)
-            if t == 0:
-                z_planes[half] = ring.tile([P, PACK, HALF], BF16, name="z_planes", tag="bf", bufs=3, align_bytes=64)
-            planes = z_planes[half]
-            nc.scalar.activation(x, x, ABS)
-            nc.scalar.activation(planes[:, t, :], x, IDENTITY, bias=dv_rows[:, b, t : t + 1])
+            magnitude = take(b_terms)
+            nc.scalar.activation(magnitude[:], x, ABS)
+            nc.scalar.activation(planes[:, t, :], magnitude[:], IDENTITY, bias=dv_rows[:, b, t : t + 1])
             if t == PACK - 1:
                 target = woven[:, b * PACK * HALF : (b + 1) * PACK * HALF]
                 nc.scalar.copy(
@@ -193,7 +260,7 @@ def tile_list_reefer_fault_board_kernel(
                 )
 
         def quantize_z(half, woven):
-            codes = keep.tile([P, 2 * HALF], U32, name="z_codes%d" % half, align_bytes=64)
+            codes = keep.tile([P, 2 * HALF], U32, name="z_codes%d" % half, tag="z_codes%d" % half, align_bytes=64)
             scales = keep.tile([P, 2 * HALF], U8, name="z_scales%d" % half, align_bytes=64)
             nc.vector.quantize_mx(codes[:].bitcast(FP8X4), scales[:], woven)
             return codes, scales
@@ -201,30 +268,41 @@ def tile_list_reefer_fault_board_kernel(
         z_store = keep.tile([P, PACK * HALF], F32, name="z_store", align_bytes=64)
         woven0 = z_store[:].bitcast(BF16)
         wd_q = {}
+        for u in range(-1, 5):
+            h_step(u)
+        wa1_woven = weave_weight_block(wa_raw1[:])
+        for b in range(2):
+            wd_raw[(1, b)] = load_weight_block(wd, 1, b)[:]
+            load_page(5 + b)
+        load_page(7)
+        list4 = load_list(offs4, "list4")
         wgo_rows = keep.tile([P, PACK, S], F32, name="wgo_rows")
-        make_h(0)
-        make_h(1)
-        wa_q.append(quantize_weight_block(wa_raw1, "wa1"))
+        load_row_weights(wgo_rows[:], wgo.rearrange("(q t) c -> q t c", t=PACK))
         x_first = {}
+        wd_woven = {}
         for s in range(SLICES):
-            if s + 2 < SLICES:
-                load_page(s + 2)
-                make_h(s + 2)
-            if s < 4:
-                a, b = divmod(s, 2)
-                wd_q[(a, b)] = quantize_weight_block(load_weight_block(wd, a, b), "wd%d" % s)
             put_h(s)
-            x_first[s] = ring.tile([P, HALF], F32, name="x", tag="x", bufs=4)
+            x_first[s] = take(x_ring)
             fetch(s, 0, x_first[s][:])
+            if s == 1:
+                wa1_codes = keep.tile([P, PASS], U32, name="wa1_codes", tag="h_single", align_bytes=64)
+                wa_q.append(quantize_weight_block(wa1_woven, wa1_codes[:], "wa1"))
+            if s in (4, 6):
+                a = (s - 4) // 2
+                wd_codes = keep.tile([P, H], U32, name="wd_codes%d" % a, tag="wgs_rows%d" % (s - PACK), align_bytes=64)
+                for b in range(2):
+                    codes = wd_codes[:, half_cols(b)]
+                    wd_q[(a, b)] = quantize_weight_block(wd_woven[(a, b)], codes, "wd%d%d" % (a, b))
+            h_step(2 * s + 5)
+            h_step(2 * s + 6)
             if s >= 1:
                 make_z(s - 1, 0, x_first[s - 1][:], woven0)
-            if s == 4:
-                list4 = load_list(offs4, "list4")
-                load_row_weights(wgo_rows, wgo, 0, PACK)
+            if 2 <= s < 6:
+                wd_woven[divmod(s - 2, 2)] = weave_weight_block(wd_raw[divmod(s - 2, 2)])
         make_z(SLICES - 1, 0, x_first[SLICES - 1][:], woven0)
 
         last_h = h_tiles[SLICES - 1]
-        x_second = [wgs_rows[:, PACK - 1, 0:HALF], wgs_rows[:, PACK - 1, HALF:S], last_h[:, 0:HALF], last_h[:, HALF:S]]
+        x_second = [wgs_rows[PACK - 1][:, 0:HALF], wgs_rows[PACK - 1][:, HALF:S], last_h[:, 0:HALF], last_h[:, HALF:S]]
         x_second = x_second + [z_store[:, u * HALF : (u + 1) * HALF] for u in range(PACK)]
         for s in range(PACK):
             fetch(s, 1, x_second[s])
@@ -232,39 +310,54 @@ def tile_list_reefer_fault_board_kernel(
         for s in range(PACK, SLICES):
             fetch(s, 1, x_second[s])
 
-        def update(s, half):
+        def update_terms(half, s):
             b, t = divmod(s, PACK)
-            cols_half = slice(half * HALF, (half + 1) * HALF)
-            ambient = ring.tile([P, HALF], F32, name="ambient", bufs=4)
-            nc.sync.dma_start(ambient[:], slice_rows(amb, s)[:, cols_half])
-            bank_b = psum.tile([P, HALF], F32, name="bank_b")
-            for j in range(HALF // P):
-                cols = slice(j * P, (j + 1) * P)
-                nc.tensor.transpose(bank_b[:, cols], ambient[:, cols], identity[:])
-            term_b = ring.tile([P, HALF], F32, name="term_b", bufs=3)
-            nc.scalar.copy(term_b[:], bank_b[:])
+            direct = (s, half) in DIRECT2
+            ambient = take(ambient_tiles)
+            nc.sync.dma_start(ambient[:], slice_rows(amb, s)[:, half_cols(half)])
+            if not direct:
+                bank_b = take(b_banks)
+                for j in range(HALF // P):
+                    cols = slice(j * P, (j + 1) * P)
+                    nc.tensor.transpose(bank_b[:, cols], ambient[:, cols], identity[:])
+                ambient = to_sbuf(bank_b, b_terms)
             z_codes, z_scales = z_q[half]
             own = slice(t * P, (t + 1) * P)
-            bank_a = psum.tile([P, HALF], F32, name="bank_a")
-            for j in range(HALF // P):
-                for a in range(2):
-                    cols = slice(a * HALF + j * P, a * HALF + (j + 1) * P)
-                    wd_codes, wd_scales = wd_q[(a, b)]
-                    nc.tensor.matmul_mx(
-                        bank_a[:, j * P : (j + 1) * P], z_codes[:, cols].bitcast(FP8X4), z_scales[:, cols],
-                        wd_codes[:, own].bitcast(FP8X4), wd_scales[:, own], start=(a == 0), stop=(a == 1),
-                    )
-            term_a = ring.tile([P, HALF], F32, name="term_a", bufs=3)
-            nc.scalar.copy(term_a[:], bank_a[:])
-            y = ring.tile([P, HALF], F32, name="y", tag="x", bufs=4)
-            add_transposed(term_a, term_b, y[:])
-            nc.vector.tensor_tensor(pages[s][:].indirect(list_half(list4, half)), y[:], wgo_rows[:, t, cols_half], MULT)
+            bank_a = take(a_banks)
+            passes = []
+            for a in range(2):
+                wd_codes, wd_scales = wd_q[(a, b)]
+                passes.append((z_codes[:, half_cols(a)], z_scales[:, half_cols(a)], wd_codes[:, own].bitcast(FP8X4), wd_scales[:, own]))
+            product(bank_a, "tokens" if direct else "weights", passes)
+            return direct, (bank_a if direct else to_sbuf(bank_a, a_terms)), ambient
 
-        second_store = ring.tile([P, 2 * PACK * HALF], BF16, name="second_store", tag="raw", align_bytes=64)
-        for s in range(SLICES):
-            update(s, 0)
-            make_z(s, 1, x_second[s], second_store[:])
-        z_q.append(quantize_z(1, second_store[:]))
-        for s in range(SLICES):
-            update(s, 1)
-            nc.sync.dma_start(slice_rows(out, s), pages[s][:])
+        def put_y(terms, half, s):
+            if (half, s) == (0, 5):
+                y = keep.tile([P, HALF], F32, name="y_single", tag="z_codes1", align_bytes=64)[:]
+            else:
+                y = take(x_ring)[:]
+            add_terms(terms, y)
+            nc.vector.tensor_tensor(
+                pages[s][:].indirect(list_half(list4, half)), y, wgo_rows[:, s % PACK, half_cols(half)], MULT
+            )
+
+        second_store = take(raw_tiles)[:].rearrange("p i c -> p (i c)").bitcast(BF16)
+        done = 0
+        terms = update_terms(0, 0)
+        for u in range(2 * SLICES):
+            half, s = divmod(u, SLICES)
+            if u == SLICES - 1:
+                put_y(terms, half, s)
+                terms = update_terms(1, 0)
+                continue
+            following = update_terms(*divmod(u + 1, SLICES)) if u + 1 < 2 * SLICES else None
+            put_y(terms, half, s)
+            terms = following
+            if half == 0:
+                for r in range(done, done + Z_AFTER[s]):
+                    make_z(r, 1, x_second[r], second_store)
+                done = done + Z_AFTER[s]
+                if done == SLICES and Z_AFTER[s] > 0:
+                    z_q.append(quantize_z(1, second_store))
+            else:
+                nc.sync.dma_start(slice_rows(out, s), pages[s][:])

@@ -26,8 +26,9 @@ HALF = 512
 SLICES = H // P
 LIST_COLS = HALF // 16
 DIRECT1 = [(0, 0), (0, 1)]
-DIRECT2 = [(0, 0), (2, 0), (0, 1)]
-Z_AFTER = [2, 1, 2, 1, 1, 1, 0, 0]
+DIRECT2 = [(0, 0), (1, 0), (0, 1)]
+STAGED_UNITS = {3: 1, 7: 0, 9: 1}
+Z_AFTER = [2, 2, 1, 1, 1, 1, 0, 0]
 
 
 def take(turns):
@@ -57,7 +58,7 @@ def tile_list_reefer_fault_board_kernel(
         b_terms = rotation(keep, "term_b", 5, [P, HALF], F32)
         h_ring = rotation(keep, "h", 3, [P, S], F32)
         x_ring = rotation(keep, "x", 4, [P, HALF], F32)
-        ambient_tiles = rotation(keep, "ambient", 4, [P, HALF], F32)
+        ambient_tiles = [keep.tile([P, HALF], F32, name="ambient%d" % u) for u in range(2 * SLICES)]
         a_banks = cycle([psum.tile([P, HALF], F32, name="bank_a%d" % n) for n in range(3)])
         b_banks = cycle([psum.tile([P, HALF], F32, name="bank_b%d" % n) for n in range(3)])
         sum_banks = cycle([psum.tile([P, HALF], F32, name="sum_bank%d" % n) for n in range(2)])
@@ -88,9 +89,9 @@ def tile_list_reefer_fault_board_kernel(
             nc.sync.dma_start(raw[:], rows.rearrange("(p i) c -> p i c", i=PACK))
             return raw
 
-        def weave_weight_block(raw):
+        def weave_weight_block(raw, copy):
             woven = take(woven_tiles)
-            nc.scalar.copy(
+            copy(
                 woven[:].rearrange("p (t m i) -> p m t i", t=PACK, i=PACK),
                 raw.rearrange("p i (m t) -> p m t i", t=PACK),
             )
@@ -105,12 +106,17 @@ def tile_list_reefer_fault_board_kernel(
             for q in range(4):
                 nc.sync.dma_start(tile[32 * q : 32 * (q + 1)], rows)
 
+        def load_ambient(units):
+            for u in units:
+                half, s = divmod(u, SLICES)
+                nc.sync.dma_start(ambient_tiles[u][:], slice_rows(amb, s)[:, half_cols(half)])
+
         pages = [keep.tile([P, T2], F32, name="page%d" % s) for s in range(SLICES)]
 
         def load_page(s):
             nc.sync.dma_start(pages[s][:], slice_rows(page0, s))
 
-        table_scales = keep.tile([P, T], U8, name="table_scales")
+        table_scales = keep.tile([P, T], U8, name="table_scales", align_bytes=64)
         nc.vector.memset(table_scales[:].bitcast(I32), 0)
         load_scale_rows(table_scales, tab_scales)
         identity = keep.tile([P, P], F32, name="identity")
@@ -148,23 +154,27 @@ def tile_list_reefer_fault_board_kernel(
         w4_codes = keep.tile([P, 2 * H], U8, name="w4_codes", align_bytes=64)
         w4_plane = keep.tile([P, H], U8, name="w4_plane", align_bytes=64)
         nc.vector.tensor_copy(
-            w4_plane[:].rearrange("p (b t m) -> p b m t", b=2, t=PACK),
-            w4_raw_scales[:].rearrange("p (b m t) -> p b m t", b=2, t=PACK),
+            w4_plane[:].rearrange("p (b t m) -> p b t m", b=2, t=PACK),
+            w4_raw_scales[:].rearrange("p (b m t) -> p b t m", b=2, t=PACK),
         )
         nc.vector.tensor_copy(
-            w4_codes[:].bitcast(U16).rearrange("p (b t m) -> p b m t", b=2, t=PACK),
-            w4_raw[:].bitcast(U16).rearrange("p (b m t) -> p b m t", b=2, t=PACK),
+            w4_codes[:].bitcast(U16).rearrange("p (b t m) -> p b t m", b=2, t=PACK),
+            w4_raw[:].bitcast(U16).rearrange("p (b m t) -> p b t m", b=2, t=PACK),
         )
         wa0_codes = keep.tile([P, PASS], U32, name="wa0_codes", align_bytes=64)
-        wa_q = [quantize_weight_block(weave_weight_block(wa_raw0[:]), wa0_codes[:], "wa0")]
+        wa_q = [quantize_weight_block(weave_weight_block(wa_raw0[:], nc.vector.tensor_copy), wa0_codes[:], "wa0")]
 
         picked = []
+        planes_picked = []
         for half in range(2):
-            words = keep.tile([P, HALF], U32, name="picked_words%d" % half, align_bytes=64)
             plane = keep.tile([P, HALF], U8, name="picked_scales%d" % half, align_bytes=64)
             nc.vector.tensor_copy(plane[:], table_scales[:].indirect(list_half(list1, half)))
-            nc.vector.tensor_copy(words[:], table_words[:].indirect(list_half(list1, half)))
-            picked.append((words, plane))
+            planes_picked.append(plane)
+        picked_words = keep.tile([P, S], U32, name="picked_words", tag="table_scales", align_bytes=64)
+        for half in range(2):
+            words = picked_words[:, half_cols(half)]
+            nc.vector.tensor_copy(words, table_words[:].indirect(list_half(list1, half)))
+            picked.append((words, planes_picked[half]))
 
         def product(bank, moving_side, passes):
             if moving_side == "tokens":
@@ -207,7 +217,12 @@ def tile_list_reefer_fault_board_kernel(
             w4_own = w4_codes[:, 2 * s * P : 2 * (s + 1) * P].bitcast(FP4X4)
             product(bank_b, side, [(words[:], plane[:], w4_own, w4_plane[:, s * P : (s + 1) * P])])
             product(bank_a, side, [(words[:], plane[:], wa_codes[:, own].bitcast(FP8X4), wa_scales[:, own])])
-            term_b = take(b_terms)
+            if 2 * s + half in STAGED_UNITS:
+                staged = woven_tiles["tiles"][STAGED_UNITS[2 * s + half]][:].bitcast(F32)
+                nc.scalar.activation(staged[:, 0:HALF], bank_b[:], ABS)
+                nc.scalar.copy(staged[:, HALF:S], bank_a[:])
+                return direct, staged[:, HALF:S], staged[:, 0:HALF]
+            term_b = b_terms["tiles"][2 * half + s % 2]
             nc.scalar.activation(term_b[:], bank_b[:], ABS)
             return direct, (bank_a if direct else to_sbuf(bank_a, a_terms)), term_b
 
@@ -231,16 +246,8 @@ def tile_list_reefer_fault_board_kernel(
                     h_tiles[s] = h_single if s == 1 else take(h_ring)
                 add_terms(h_terms[u], h_tiles[s][:, half_cols(half)])
 
-        def put_h(s):
-            t = s % PACK
-            if s == 0:
-                for half in range(2):
-                    cols = half_cols(half)
-                    nc.vector.tensor_tensor(
-                        pages[s][:].indirect(list_half(list2, half)), h_tiles[s][:, cols], wgs_rows[t][:, cols], MULT
-                    )
-            else:
-                nc.vector.tensor_tensor(pages[s][:].indirect(list2[:]), h_tiles[s][:], wgs_rows[t][:], MULT)
+        def put_h(s, offsets, cols):
+            nc.vector.tensor_tensor(pages[s][:].indirect(offsets), h_tiles[s][:, cols], wgs_rows[s % PACK][:, cols], MULT)
 
         def fetch(s, half, x):
             nc.vector.tensor_copy(x, pages[s][:].indirect(list_half(list3, half)))
@@ -249,7 +256,7 @@ def tile_list_reefer_fault_board_kernel(
 
         def make_z(s, half, x, woven):
             b, t = divmod(s, PACK)
-            magnitude = take(b_terms)
+            magnitude = b_terms["tiles"][(s + 1) % 2] if half == 0 else take(b_terms)
             nc.scalar.activation(magnitude[:], x, ABS)
             nc.scalar.activation(planes[:, t, :], magnitude[:], IDENTITY, bias=dv_rows[:, b, t : t + 1])
             if t == PACK - 1:
@@ -265,24 +272,39 @@ def tile_list_reefer_fault_board_kernel(
             nc.vector.quantize_mx(codes[:].bitcast(FP8X4), scales[:], woven)
             return codes, scales
 
+        def transpose_ambient(unit, bank):
+            ambient = ambient_tiles[unit]
+            for j in range(HALF // P):
+                cols = slice(j * P, (j + 1) * P)
+                nc.tensor.transpose(bank[:, cols], ambient[:, cols], identity[:])
+            nc.scalar.copy(ambient[:], bank[:])
+
+        to_transpose = [u for u in range(2 * SLICES) if (u % SLICES, u // SLICES) not in DIRECT2]
+
         z_store = keep.tile([P, PACK * HALF], F32, name="z_store", align_bytes=64)
         woven0 = z_store[:].bitcast(BF16)
         wd_q = {}
         for u in range(-1, 5):
             h_step(u)
-        wa1_woven = weave_weight_block(wa_raw1[:])
-        for b in range(2):
-            wd_raw[(1, b)] = load_weight_block(wd, 1, b)[:]
-            load_page(5 + b)
+            if 0 <= u < 2:
+                put_h(0, list_half(list2, u), half_cols(u))
+        wa1_woven = weave_weight_block(wa_raw1[:], nc.scalar.copy)
+        load_ambient(to_transpose[0:4])
+        wd_raw[(1, 0)] = load_weight_block(wd, 1, 0)[:]
+        load_ambient(to_transpose[4:8])
+        load_page(5)
+        wd_raw[(1, 1)] = load_weight_block(wd, 1, 1)[:]
+        load_page(6)
+        load_ambient([u for u in range(2 * SLICES) if u not in to_transpose[0:8]])
         load_page(7)
         list4 = load_list(offs4, "list4")
-        wgo_rows = keep.tile([P, PACK, S], F32, name="wgo_rows")
-        load_row_weights(wgo_rows[:], wgo.rearrange("(q t) c -> q t c", t=PACK))
         x_first = {}
+        spare = keep.tile([P, HALF], F32, name="spare", tag="z_codes1", align_bytes=64)
         wd_woven = {}
         for s in range(SLICES):
-            put_h(s)
-            x_first[s] = take(x_ring)
+            if s > 0:
+                put_h(s, list2[:], slice(0, S))
+            x_first[s] = spare if s == SLICES - 1 else take(x_ring)
             fetch(s, 0, x_first[s][:])
             if s == 1:
                 wa1_codes = keep.tile([P, PASS], U32, name="wa1_codes", tag="h_single", align_bytes=64)
@@ -293,12 +315,21 @@ def tile_list_reefer_fault_board_kernel(
                 for b in range(2):
                     codes = wd_codes[:, half_cols(b)]
                     wd_q[(a, b)] = quantize_weight_block(wd_woven[(a, b)], codes, "wd%d%d" % (a, b))
-            h_step(2 * s + 5)
-            h_step(2 * s + 6)
+            for u in (2 * s + 5, 2 * s + 6):
+                h_step(u)
+                if 12 <= u < 16:
+                    for unit in to_transpose[2 * (u - 12) : 2 * (u - 11)]:
+                        transpose_ambient(unit, take(sum_banks))
             if s >= 1:
                 make_z(s - 1, 0, x_first[s - 1][:], woven0)
             if 2 <= s < 6:
-                wd_woven[divmod(s - 2, 2)] = weave_weight_block(wd_raw[divmod(s - 2, 2)])
+                wd_woven[divmod(s - 2, 2)] = weave_weight_block(wd_raw[divmod(s - 2, 2)], nc.scalar.copy)
+            if s == 3:
+                wgo_rows = keep.tile([P, PACK, S], F32, name="wgo_rows", tag="wide")
+                load_row_weights(wgo_rows[:], wgo.rearrange("(q t) c -> q t c", t=PACK))
+            if s == 5:
+                for n, unit in enumerate(to_transpose[8:]):
+                    transpose_ambient(unit, take(b_banks if n % 2 == 0 else a_banks))
         make_z(SLICES - 1, 0, x_first[SLICES - 1][:], woven0)
 
         last_h = h_tiles[SLICES - 1]
@@ -313,14 +344,7 @@ def tile_list_reefer_fault_board_kernel(
         def update_terms(half, s):
             b, t = divmod(s, PACK)
             direct = (s, half) in DIRECT2
-            ambient = take(ambient_tiles)
-            nc.sync.dma_start(ambient[:], slice_rows(amb, s)[:, half_cols(half)])
-            if not direct:
-                bank_b = take(b_banks)
-                for j in range(HALF // P):
-                    cols = slice(j * P, (j + 1) * P)
-                    nc.tensor.transpose(bank_b[:, cols], ambient[:, cols], identity[:])
-                ambient = to_sbuf(bank_b, b_terms)
+            ambient = ambient_tiles[half * SLICES + s]
             z_codes, z_scales = z_q[half]
             own = slice(t * P, (t + 1) * P)
             bank_a = take(a_banks)
@@ -329,13 +353,10 @@ def tile_list_reefer_fault_board_kernel(
                 wd_codes, wd_scales = wd_q[(a, b)]
                 passes.append((z_codes[:, half_cols(a)], z_scales[:, half_cols(a)], wd_codes[:, own].bitcast(FP8X4), wd_scales[:, own]))
             product(bank_a, "tokens" if direct else "weights", passes)
-            return direct, (bank_a if direct else to_sbuf(bank_a, a_terms)), ambient
+            return direct, (bank_a if direct else to_sbuf(bank_a, b_terms)), ambient
 
         def put_y(terms, half, s):
-            if (half, s) == (0, 5):
-                y = keep.tile([P, HALF], F32, name="y_single", tag="z_codes1", align_bytes=64)[:]
-            else:
-                y = take(x_ring)[:]
+            y = spare[:] if (half, s) == (0, 5) else take(x_ring)[:]
             add_terms(terms, y)
             nc.vector.tensor_tensor(
                 pages[s][:].indirect(list_half(list4, half)), y, wgo_rows[:, s % PACK, half_cols(half)], MULT
@@ -357,7 +378,7 @@ def tile_list_reefer_fault_board_kernel(
                 for r in range(done, done + Z_AFTER[s]):
                     make_z(r, 1, x_second[r], second_store)
                 done = done + Z_AFTER[s]
-                if done == SLICES and Z_AFTER[s] > 0:
+                if s == 5:
                     z_q.append(quantize_z(1, second_store))
             else:
                 nc.sync.dma_start(slice_rows(out, s), pages[s][:])

@@ -116,13 +116,15 @@ def tile_list_reefer_fault_board_kernel(
         def load_page(s):
             nc.sync.dma_start(pages[s][:], slice_rows(page0, s))
 
-        table_scales = keep.tile([P, T], U8, name="table_scales", align_bytes=64)
+        table_scales = keep.tile([P, T], U8, name="table_scales")
         nc.vector.memset(table_scales[:].bitcast(I32), 0)
         load_scale_rows(table_scales, tab_scales)
         identity = keep.tile([P, P], F32, name="identity")
         make_identity(nc, identity[:])
 
         list1 = load_list(offs, "list1")
+        table_words = keep.tile([P, T], U32, name="table_words", tag="wide")
+        nc.sync.dma_start(table_words[:].bitcast(I32), tab_words[0].rearrange("p c i -> p (c i)").bitcast(I32))
         w4_raw_scales = keep.tile([P, H], U8, name="w4_raw_scales")
         for q in range(4):
             rows = w4_scales[0, 4 * q : 4 * q + 4, :].bitcast(I32)
@@ -130,8 +132,6 @@ def tile_list_reefer_fault_board_kernel(
         w4_raw = keep.tile([P, 2 * H], U8, name="w4_raw")
         nc.sync.dma_start(w4_raw[:].bitcast(I32), w4_words[0].bitcast(I32))
         wa_raw0 = load_weight_block(wa, 0, 0)
-        table_words = keep.tile([P, T], U32, name="table_words", tag="wide")
-        nc.sync.dma_start(table_words[:].bitcast(I32), tab_words[0].rearrange("p c i -> p (c i)").bitcast(I32))
         load_page(0)
         list2 = load_list(offs2, "list2")
         wgs_rows = [keep.tile([P, S], F32, name="wgs_rows%d" % t, align_bytes=64) for t in range(PACK)]
@@ -162,19 +162,23 @@ def tile_list_reefer_fault_board_kernel(
             w4_raw[:].bitcast(U16).rearrange("p (b m t) -> p b t m", b=2, t=PACK),
         )
         wa0_codes = keep.tile([P, PASS], U32, name="wa0_codes", align_bytes=64)
-        wa_q = [quantize_weight_block(weave_weight_block(wa_raw0[:], nc.vector.tensor_copy), wa0_codes[:], "wa0")]
+        wa0_scales = keep.tile([P, PASS], U8, name="wa0_scales", align_bytes=64)
+        wa0_woven = take(woven_tiles)
+        wa0_dealt = wa_raw0[:].rearrange("p i (m t) -> p m t i", t=PACK)
+        for first, count in ((0, 1), (1, PACK - 1)):
+            part = wa0_woven[:, first * PASS : (first + count) * PASS]
+            nc.scalar.copy(part.rearrange("p (t m i) -> p m t i", t=count, i=PACK), wa0_dealt[:, :, first : first + count, :])
+            cols = slice(first * P, (first + count) * P)
+            nc.vector.quantize_mx(wa0_codes[:, cols].bitcast(FP8X4), wa0_scales[:, cols], part)
+        wa_q = [(wa0_codes[:], wa0_scales)]
 
         picked = []
-        planes_picked = []
         for half in range(2):
+            words = keep.tile([P, HALF], U32, name="picked_words%d" % half, align_bytes=64)
             plane = keep.tile([P, HALF], U8, name="picked_scales%d" % half, align_bytes=64)
+            nc.vector.tensor_copy(words[:], table_words[:].indirect(list_half(list1, half)))
             nc.vector.tensor_copy(plane[:], table_scales[:].indirect(list_half(list1, half)))
-            planes_picked.append(plane)
-        picked_words = keep.tile([P, S], U32, name="picked_words", tag="table_scales", align_bytes=64)
-        for half in range(2):
-            words = picked_words[:, half_cols(half)]
-            nc.vector.tensor_copy(words, table_words[:].indirect(list_half(list1, half)))
-            picked.append((words, planes_picked[half]))
+            picked.append((words, plane))
 
         def product(bank, moving_side, passes):
             if moving_side == "tokens":

@@ -24,11 +24,19 @@ PACK = 4
 PASS = P * PACK
 HALF = 512
 SLICES = H // P
+UNITS = 2 * SLICES
 LIST_COLS = HALF // 16
-DIRECT1 = [(0, 0), (0, 1)]
-DIRECT2 = [(0, 0), (1, 0), (0, 1)]
-STAGED_UNITS = {3: 1, 7: 0, 9: 1}
-Z_AFTER = [2, 2, 1, 1, 1, 1, 0, 0]
+
+TERMS_IN_STAGING = {3: 1, 7: 0, 9: 1}
+AMB_FROM_SUM = UNITS - 4
+AMB_BEHIND_SUMS = 8
+AMB_IN_FIRST_STAGE = 12
+QUANTISE_BEHIND = 5
+UNITS_WITH_TWO = SLICES - (QUANTISE_BEHIND + 1)
+
+
+def in_turn(tiles):
+    return {"tiles": tiles, "taken": 0}
 
 
 def take(turns):
@@ -37,8 +45,17 @@ def take(turns):
     return turns["tiles"][count % len(turns["tiles"])]
 
 
-def cycle(tiles):
-    return {"tiles": tiles, "taken": 0}
+def half_cols(half):
+    return slice(half * HALF, (half + 1) * HALF)
+
+
+def list_half(tile, half):
+    return tile[:, half * LIST_COLS : (half + 1) * LIST_COLS]
+
+
+def slice_rows(matrix, s):
+    b, t = divmod(s, PACK)
+    return matrix[PASS * b : PASS * (b + 1), :].rearrange("(p t) c -> t p c", t=PACK)[t]
 
 
 def tile_list_reefer_fault_board_kernel(
@@ -49,39 +66,31 @@ def tile_list_reefer_fault_board_kernel(
         keep = ctx.enter_context(tc.tile_pool(name="keep", bufs=1))
         psum = ctx.enter_context(tc.psum_pool(name="psum", bufs=1))
 
-        def rotation(pool, name, count, shape, dtype):
-            return cycle([pool.tile(shape, dtype, name="%s%d" % (name, n), align_bytes=64) for n in range(count)])
+        def sbuf_in_turn(name, count, shape, dtype):
+            return in_turn([keep.tile(shape, dtype, name="%s%d" % (name, n), align_bytes=64) for n in range(count)])
 
-        raw_tiles = rotation(keep, "raw", 2, [P, PACK, PASS], F32)
-        woven_tiles = rotation(keep, "woven", 2, [P, PACK * PASS], BF16)
-        a_terms = rotation(keep, "term_a", 3, [P, HALF], F32)
-        b_terms = rotation(keep, "term_b", 5, [P, HALF], F32)
-        h_ring = rotation(keep, "h", 3, [P, S], F32)
-        x_ring = rotation(keep, "x", 4, [P, HALF], F32)
-        ambient_tiles = [keep.tile([P, HALF], F32, name="ambient%d" % u) for u in range(2 * SLICES)]
-        a_banks = cycle([psum.tile([P, HALF], F32, name="bank_a%d" % n) for n in range(3)])
-        b_banks = cycle([psum.tile([P, HALF], F32, name="bank_b%d" % n) for n in range(3)])
-        sum_banks = cycle([psum.tile([P, HALF], F32, name="sum_bank%d" % n) for n in range(2)])
+        def banks_in_turn(name, count):
+            return in_turn([psum.tile([P, HALF], F32, name="%s%d" % (name, n)) for n in range(count)])
+
+        raw_tiles = sbuf_in_turn("raw", 2, [P, PACK, PASS], F32)
+        staging_tiles = sbuf_in_turn("staging", 2, [P, PACK * PASS], BF16)
+        a_terms = sbuf_in_turn("term_a", 3, [P, HALF], F32)
+        b_terms = sbuf_in_turn("term_b", 5, [P, HALF], F32)
+        h_ring = sbuf_in_turn("h", 3, [P, S], F32)
+        x_ring = sbuf_in_turn("x", 4, [P, HALF], F32)
+        amb_tiles = [keep.tile([P, HALF], F32, name="amb%d" % u) for u in range(UNITS)]
+        a_banks = banks_in_turn("bank_a", 3)
+        b_banks = banks_in_turn("bank_b", 3)
+        sum_banks = banks_in_turn("sum_bank", 2)
+        pages = [keep.tile([P, T2], F32, name="page%d" % s) for s in range(SLICES)]
 
         def load_list(source, name):
             tile = keep.tile([P, S // 16], U16, name=name)
             nc.sync.dma_start(tile[:], source)
             return tile
 
-        def list_half(tile, half):
-            return tile[:, half * LIST_COLS : (half + 1) * LIST_COLS]
-
-        def half_cols(half):
-            return slice(half * HALF, (half + 1) * HALF)
-
-        def load_scale_rows(tile, source):
-            for q in range(4):
-                rows = source[0, 4 * q : 4 * q + 4, :].bitcast(I32)
-                nc.gpsimd.dma_start(tile[32 * q : 32 * q + 4, :].bitcast(I32), rows)
-
-        def slice_rows(matrix, s):
-            b, t = divmod(s, PACK)
-            return matrix[PASS * b : PASS * (b + 1), :].rearrange("(p t) c -> t p c", t=PACK)[t]
+        def load_page(s):
+            nc.sync.dma_start(pages[s][:], slice_rows(page0, s))
 
         def load_weight_block(matrix, a, b):
             raw = take(raw_tiles)
@@ -89,36 +98,20 @@ def tile_list_reefer_fault_board_kernel(
             nc.sync.dma_start(raw[:], rows.rearrange("(p i) c -> p i c", i=PACK))
             return raw
 
-        def weave_weight_block(raw, copy):
-            woven = take(woven_tiles)
-            copy(
-                woven[:].rearrange("p (t m i) -> p m t i", t=PACK, i=PACK),
-                raw.rearrange("p i (m t) -> p m t i", t=PACK),
-            )
-            return woven
-
-        def quantize_weight_block(woven, codes, name):
-            scales = keep.tile([P, PASS], U8, name=name + "_scales", align_bytes=64)
-            nc.vector.quantize_mx(codes.bitcast(FP8X4), scales[:], woven[:])
-            return codes, scales
-
-        def load_row_weights(tile, rows):
+        def load_on_each_quadrant(tile, rows):
             for q in range(4):
                 nc.sync.dma_start(tile[32 * q : 32 * (q + 1)], rows)
 
-        def load_ambient(units):
+        def load_amb(units):
             for u in units:
                 half, s = divmod(u, SLICES)
-                nc.sync.dma_start(ambient_tiles[u][:], slice_rows(amb, s)[:, half_cols(half)])
-
-        pages = [keep.tile([P, T2], F32, name="page%d" % s) for s in range(SLICES)]
-
-        def load_page(s):
-            nc.sync.dma_start(pages[s][:], slice_rows(page0, s))
+                nc.sync.dma_start(amb_tiles[u][:], slice_rows(amb, s)[:, half_cols(half)])
 
         table_scales = keep.tile([P, T], U8, name="table_scales")
         nc.vector.memset(table_scales[:].bitcast(I32), 0)
-        load_scale_rows(table_scales, tab_scales)
+        for q in range(4):
+            rows = tab_scales[0, 4 * q : 4 * q + 4, :].bitcast(I32)
+            nc.gpsimd.dma_start(table_scales[32 * q : 32 * q + 4, :].bitcast(I32), rows)
         identity = keep.tile([P, P], F32, name="identity")
         make_identity(nc, identity[:])
 
@@ -137,55 +130,69 @@ def tile_list_reefer_fault_board_kernel(
         wgs_rows = [keep.tile([P, S], F32, name="wgs_rows%d" % t, align_bytes=64) for t in range(PACK)]
         wgs_dealt = wgs.rearrange("(q t) c -> t q c", t=PACK)
         for half in range(2):
-            load_row_weights(wgs_rows[0][:, half_cols(half)], wgs_dealt[0][:, half_cols(half)])
+            load_on_each_quadrant(wgs_rows[0][:, half_cols(half)], wgs_dealt[0][:, half_cols(half)])
         list3 = load_list(offs3, "list3")
-        for s in range(1, PACK):
+        load_page(1)
+        load_on_each_quadrant(wgs_rows[1][:], wgs_dealt[1])
+        wa_raw1 = load_weight_block(wa, 0, 1)
+        dv_rows = keep.tile([P, 2, PACK], F32, name="dv_rows")
+        nc.sync.dma_start(dv_rows[:], dv.rearrange("(b p t) -> p b t", b=2, t=PACK))
+        for s in range(2, PACK):
             load_page(s)
-            load_row_weights(wgs_rows[s][:], wgs_dealt[s])
-            if s == 1:
-                wa_raw1 = load_weight_block(wa, 0, 1)
-                dv_rows = keep.tile([P, 2, PACK], F32, name="dv_rows")
-                nc.sync.dma_start(dv_rows[:], dv.rearrange("(b p t) -> p b t", b=2, t=PACK))
+            load_on_each_quadrant(wgs_rows[s][:], wgs_dealt[s])
         wd_wide = keep.tile([P, PACK, H], F32, name="wd_wide", tag="wide")
         nc.sync.dma_start(wd_wide[:], wd[0:PASS, :].rearrange("(p i) c -> p i c", i=PACK))
-        load_page(4)
+        load_page(PACK)
         wd_raw = {(0, 0): wd_wide[:, :, 0:PASS], (0, 1): wd_wide[:, :, PASS:H]}
 
         w4_codes = keep.tile([P, 2 * H], U8, name="w4_codes", align_bytes=64)
-        w4_plane = keep.tile([P, H], U8, name="w4_plane", align_bytes=64)
+        w4_dealt_scales = keep.tile([P, H], U8, name="w4_dealt_scales", align_bytes=64)
         nc.vector.tensor_copy(
-            w4_plane[:].rearrange("p (b t m) -> p b t m", b=2, t=PACK),
+            w4_dealt_scales[:].rearrange("p (b t m) -> p b t m", b=2, t=PACK),
             w4_raw_scales[:].rearrange("p (b m t) -> p b t m", b=2, t=PACK),
         )
         nc.vector.tensor_copy(
             w4_codes[:].bitcast(U16).rearrange("p (b t m) -> p b t m", b=2, t=PACK),
             w4_raw[:].bitcast(U16).rearrange("p (b m t) -> p b t m", b=2, t=PACK),
         )
+
+        def cast_columns(staging, raw, first, count):
+            part = staging[:, first * PASS : (first + count) * PASS]
+            dealt = raw.rearrange("p i (m t) -> p m t i", t=PACK)[:, :, first : first + count, :]
+            nc.scalar.copy(part.rearrange("p (t m i) -> p m t i", t=count, i=PACK), dealt)
+            return part
+
+        def cast_weight_block(raw):
+            return cast_columns(take(staging_tiles), raw, 0, PACK)
+
+        def quantize_weight_block(staged, codes, name):
+            scales = keep.tile([P, PASS], U8, name=name + "_scales", align_bytes=64)
+            nc.vector.quantize_mx(codes.bitcast(FP8X4), scales[:], staged)
+            return codes, scales
+
         wa0_codes = keep.tile([P, PASS], U32, name="wa0_codes", align_bytes=64)
         wa0_scales = keep.tile([P, PASS], U8, name="wa0_scales", align_bytes=64)
-        wa0_woven = take(woven_tiles)
-        wa0_dealt = wa_raw0[:].rearrange("p i (m t) -> p m t i", t=PACK)
+        wa0_staging = take(staging_tiles)
         for first, count in ((0, 1), (1, PACK - 1)):
-            part = wa0_woven[:, first * PASS : (first + count) * PASS]
-            nc.scalar.copy(part.rearrange("p (t m i) -> p m t i", t=count, i=PACK), wa0_dealt[:, :, first : first + count, :])
+            part = cast_columns(wa0_staging, wa_raw0[:], first, count)
             cols = slice(first * P, (first + count) * P)
             nc.vector.quantize_mx(wa0_codes[:, cols].bitcast(FP8X4), wa0_scales[:, cols], part)
-        wa_q = [(wa0_codes[:], wa0_scales)]
+        wa_mx = [(wa0_codes[:], wa0_scales)]
 
         picked = []
         for half in range(2):
             words = keep.tile([P, HALF], U32, name="picked_words%d" % half, align_bytes=64)
-            plane = keep.tile([P, HALF], U8, name="picked_scales%d" % half, align_bytes=64)
+            scales = keep.tile([P, HALF], U8, name="picked_scales%d" % half, align_bytes=64)
             nc.vector.tensor_copy(words[:], table_words[:].indirect(list_half(list1, half)))
-            nc.vector.tensor_copy(plane[:], table_scales[:].indirect(list_half(list1, half)))
-            picked.append((words, plane))
+            nc.vector.tensor_copy(scales[:], table_scales[:].indirect(list_half(list1, half)))
+            picked.append((words, scales))
 
-        def product(bank, moving_side, passes):
-            if moving_side == "tokens":
+        def product(bank, transposed, passes):
+            last = len(passes) - 1
+            if not transposed:
                 for a, (codes, scales, w_codes, w_scales) in enumerate(passes):
                     nc.tensor.matmul_mx(
-                        bank[:], w_codes, w_scales, codes.bitcast(FP8X4), scales,
-                        start=(a == 0), stop=(a == len(passes) - 1),
+                        bank[:], w_codes, w_scales, codes.bitcast(FP8X4), scales, start=(a == 0), stop=(a == last)
                     )
                 return
             for j in range(HALF // P):
@@ -193,8 +200,13 @@ def tile_list_reefer_fault_board_kernel(
                 for a, (codes, scales, w_codes, w_scales) in enumerate(passes):
                     nc.tensor.matmul_mx(
                         bank[:, cols], codes[:, cols].bitcast(FP8X4), scales[:, cols], w_codes, w_scales,
-                        start=(a == 0), stop=(a == len(passes) - 1),
+                        start=(a == 0), stop=(a == last),
                     )
+
+        def to_sbuf(bank, terms):
+            term = take(terms)
+            nc.scalar.copy(term[:], bank[:])
+            return term
 
         def add_transposed(first, second, result):
             bank = take(sum_banks)
@@ -204,107 +216,99 @@ def tile_list_reefer_fault_board_kernel(
                 nc.tensor.matmul(bank[:, cols], second[:, cols], identity[:], start=False, stop=True, is_transpose=True)
             nc.scalar.copy(result, bank[:])
 
-        def to_sbuf(bank, terms):
-            term = take(terms)
-            nc.scalar.copy(term[:], bank[:])
-            return term
-
-        def feature_terms(s, half):
+        def h_terms_of(u):
+            s, half = divmod(u, 2)
             b, t = divmod(s, PACK)
-            words, plane = picked[half]
-            wa_codes, wa_scales = wa_q[b]
+            words, scales = picked[half]
+            wa_codes, wa_scales = wa_mx[b]
             own = slice(t * P, (t + 1) * P)
-            direct = (s, half) in DIRECT1
-            side = "tokens" if direct else "weights"
             bank_a = take(a_banks)
             bank_b = take(b_banks)
             w4_own = w4_codes[:, 2 * s * P : 2 * (s + 1) * P].bitcast(FP4X4)
-            product(bank_b, side, [(words[:], plane[:], w4_own, w4_plane[:, s * P : (s + 1) * P])])
-            product(bank_a, side, [(words[:], plane[:], wa_codes[:, own].bitcast(FP8X4), wa_scales[:, own])])
-            if 2 * s + half in STAGED_UNITS:
-                staged = woven_tiles["tiles"][STAGED_UNITS[2 * s + half]][:].bitcast(F32)
+            product(bank_b, s > 0, [(words[:], scales[:], w4_own, w4_dealt_scales[:, s * P : (s + 1) * P])])
+            product(bank_a, s > 0, [(words[:], scales[:], wa_codes[:, own].bitcast(FP8X4), wa_scales[:, own])])
+            if u in TERMS_IN_STAGING:
+                staged = staging_tiles["tiles"][TERMS_IN_STAGING[u]][:].bitcast(F32)
                 nc.scalar.activation(staged[:, 0:HALF], bank_b[:], ABS)
                 nc.scalar.copy(staged[:, HALF:S], bank_a[:])
-                return direct, staged[:, HALF:S], staged[:, 0:HALF]
+                return staged[:, HALF:S], staged[:, 0:HALF]
             term_b = b_terms["tiles"][2 * half + s % 2]
             nc.scalar.activation(term_b[:], bank_b[:], ABS)
-            return direct, (bank_a if direct else to_sbuf(bank_a, a_terms)), term_b
-
-        def add_terms(terms, result):
-            direct, term_a, term_b = terms
-            if direct:
-                nc.vector.tensor_tensor(result, term_a[:], term_b[:], ADD)
-            else:
-                add_transposed(term_a, term_b, result)
+            return (to_sbuf(bank_a, a_terms) if s > 0 else bank_a), term_b
 
         h_tiles = {}
         h_single = keep.tile([P, S], F32, name="h_single", align_bytes=64)
         h_terms = {}
 
         def h_step(u):
-            if u + 1 < 2 * SLICES:
-                h_terms[u + 1] = feature_terms(*divmod(u + 1, 2))
-            if 0 <= u < 2 * SLICES:
-                s, half = divmod(u, 2)
-                if half == 0:
-                    h_tiles[s] = h_single if s == 1 else take(h_ring)
-                add_terms(h_terms[u], h_tiles[s][:, half_cols(half)])
+            if u + 1 < UNITS:
+                h_terms[u + 1] = h_terms_of(u + 1)
+            s, half = divmod(u, 2)
+            if half == 0:
+                h_tiles[s] = h_single if s == 1 else take(h_ring)
+            term_a, term_b = h_terms[u]
+            if s == 0:
+                nc.vector.tensor_tensor(h_tiles[s][:, half_cols(half)], term_a[:], term_b[:], ADD)
+            else:
+                add_transposed(term_a, term_b, h_tiles[s][:, half_cols(half)])
 
         def put_h(s, offsets, cols):
-            nc.vector.tensor_tensor(pages[s][:].indirect(offsets), h_tiles[s][:, cols], wgs_rows[s % PACK][:, cols], MULT)
+            h, weights = h_tiles[s][:, cols], wgs_rows[s % PACK][:, cols]
+            nc.vector.tensor_tensor(pages[s][:].indirect(offsets), h, weights, MULT)
 
         def fetch(s, half, x):
             nc.vector.tensor_copy(x, pages[s][:].indirect(list_half(list3, half)))
 
-        planes = keep.tile([P, PACK, HALF], BF16, name="z_planes")
+        z_rows = keep.tile([P, PACK, HALF], BF16, name="z_rows")
 
-        def make_z(s, half, x, woven):
+        def make_z(s, half, x, z_words):
             b, t = divmod(s, PACK)
             magnitude = b_terms["tiles"][(s + 1) % 2] if half == 0 else take(b_terms)
             nc.scalar.activation(magnitude[:], x, ABS)
-            nc.scalar.activation(planes[:, t, :], magnitude[:], IDENTITY, bias=dv_rows[:, b, t : t + 1])
+            nc.scalar.activation(z_rows[:, t, :], magnitude[:], IDENTITY, bias=dv_rows[:, b, t : t + 1])
             if t == PACK - 1:
-                target = woven[:, b * PACK * HALF : (b + 1) * PACK * HALF]
+                target = z_words[:, b * PACK * HALF : (b + 1) * PACK * HALF]
                 nc.scalar.copy(
                     target.rearrange("p (c i t) -> p c t i", i=4, t=PACK),
-                    planes[:].rearrange("p t (c i) -> p c t i", i=4),
+                    z_rows[:].rearrange("p t (c i) -> p c t i", i=4),
                 )
 
-        def quantize_z(half, woven):
+        def quantize_z(half, z_words):
             codes = keep.tile([P, 2 * HALF], U32, name="z_codes%d" % half, tag="z_codes%d" % half, align_bytes=64)
             scales = keep.tile([P, 2 * HALF], U8, name="z_scales%d" % half, align_bytes=64)
-            nc.vector.quantize_mx(codes[:].bitcast(FP8X4), scales[:], woven)
+            nc.vector.quantize_mx(codes[:].bitcast(FP8X4), scales[:], z_words)
             return codes, scales
 
-        def transpose_ambient(unit, bank):
-            ambient = ambient_tiles[unit]
+        def transpose_amb(u, bank):
             for j in range(HALF // P):
                 cols = slice(j * P, (j + 1) * P)
-                nc.tensor.transpose(bank[:, cols], ambient[:, cols], identity[:])
-            nc.scalar.copy(ambient[:], bank[:])
-
-        to_transpose = [u for u in range(2 * SLICES) if (u % SLICES, u // SLICES) not in DIRECT2]
+                nc.tensor.transpose(bank[:, cols], amb_tiles[u][:, cols], identity[:])
+            nc.scalar.copy(amb_tiles[u][:], bank[:])
 
         z_store = keep.tile([P, PACK * HALF], F32, name="z_store", align_bytes=64)
-        woven0 = z_store[:].bitcast(BF16)
-        wd_q = {}
-        for u in range(-1, 5):
+        z_words0 = z_store[:].bitcast(BF16)
+        h_terms[0] = h_terms_of(0)
+        ahead = 5
+        for u in range(ahead):
             h_step(u)
-            if 0 <= u < 2:
+            if u < 2:
                 put_h(0, list_half(list2, u), half_cols(u))
-        wa1_woven = weave_weight_block(wa_raw1[:], nc.scalar.copy)
-        load_ambient(to_transpose[0:4])
+        wa1_staged = cast_weight_block(wa_raw1[:])
+
+        load_amb(range(0, AMB_BEHIND_SUMS // 2))
         wd_raw[(1, 0)] = load_weight_block(wd, 1, 0)[:]
-        load_ambient(to_transpose[4:8])
+        load_amb(range(AMB_BEHIND_SUMS // 2, AMB_BEHIND_SUMS))
         load_page(5)
         wd_raw[(1, 1)] = load_weight_block(wd, 1, 1)[:]
         load_page(6)
-        load_ambient([u for u in range(2 * SLICES) if u not in to_transpose[0:8]])
+        load_amb(range(AMB_BEHIND_SUMS, UNITS))
         load_page(7)
         list4 = load_list(offs4, "list4")
-        x_first = {}
+
         spare = keep.tile([P, HALF], F32, name="spare", tag="z_codes1", align_bytes=64)
-        wd_woven = {}
+        x_first = {}
+        wd_staged = {}
+        wd_mx = {}
         for s in range(SLICES):
             if s > 0:
                 put_h(s, list2[:], slice(0, S))
@@ -312,77 +316,77 @@ def tile_list_reefer_fault_board_kernel(
             fetch(s, 0, x_first[s][:])
             if s == 1:
                 wa1_codes = keep.tile([P, PASS], U32, name="wa1_codes", tag="h_single", align_bytes=64)
-                wa_q.append(quantize_weight_block(wa1_woven, wa1_codes[:], "wa1"))
-            if s in (4, 6):
-                a = (s - 4) // 2
+                wa_mx.append(quantize_weight_block(wa1_staged, wa1_codes[:], "wa1"))
+            if s in (PACK, PACK + 2):
+                a = (s - PACK) // 2
                 wd_codes = keep.tile([P, H], U32, name="wd_codes%d" % a, tag="wgs_rows%d" % (s - PACK), align_bytes=64)
                 for b in range(2):
                     codes = wd_codes[:, half_cols(b)]
-                    wd_q[(a, b)] = quantize_weight_block(wd_woven[(a, b)], codes, "wd%d%d" % (a, b))
-            for u in (2 * s + 5, 2 * s + 6):
+                    wd_mx[(a, b)] = quantize_weight_block(wd_staged[(a, b)], codes, "wd%d%d" % (a, b))
+            for u in range(ahead + 2 * s, min(ahead + 2 * s + 2, UNITS)):
                 h_step(u)
-                if 12 <= u < 16:
-                    for unit in to_transpose[2 * (u - 12) : 2 * (u - 11)]:
-                        transpose_ambient(unit, take(sum_banks))
+                if u >= AMB_FROM_SUM:
+                    for n in range(2 * (u - AMB_FROM_SUM), 2 * (u - AMB_FROM_SUM) + 2):
+                        transpose_amb(n, take(sum_banks))
             if s >= 1:
-                make_z(s - 1, 0, x_first[s - 1][:], woven0)
+                make_z(s - 1, 0, x_first[s - 1][:], z_words0)
             if 2 <= s < 6:
-                wd_woven[divmod(s - 2, 2)] = weave_weight_block(wd_raw[divmod(s - 2, 2)], nc.scalar.copy)
+                wd_staged[divmod(s - 2, 2)] = cast_weight_block(wd_raw[divmod(s - 2, 2)])
             if s == 3:
                 wgo_rows = keep.tile([P, PACK, S], F32, name="wgo_rows", tag="wide")
-                load_row_weights(wgo_rows[:], wgo.rearrange("(q t) c -> q t c", t=PACK))
+                load_on_each_quadrant(wgo_rows[:], wgo.rearrange("(q t) c -> q t c", t=PACK))
             if s == 5:
-                for n, unit in enumerate(to_transpose[8:]):
-                    transpose_ambient(unit, take(b_banks if n % 2 == 0 else a_banks))
-        make_z(SLICES - 1, 0, x_first[SLICES - 1][:], woven0)
+                for u in range(AMB_BEHIND_SUMS, AMB_IN_FIRST_STAGE):
+                    transpose_amb(u, take(b_banks if u % 2 == 0 else a_banks))
+        make_z(SLICES - 1, 0, x_first[SLICES - 1][:], z_words0)
 
-        last_h = h_tiles[SLICES - 1]
-        x_second = [wgs_rows[PACK - 1][:, 0:HALF], wgs_rows[PACK - 1][:, HALF:S], last_h[:, 0:HALF], last_h[:, HALF:S]]
-        x_second = x_second + [z_store[:, u * HALF : (u + 1) * HALF] for u in range(PACK)]
+        last_wgs, last_h = wgs_rows[PACK - 1], h_tiles[SLICES - 1]
+        x_second = [tile[:, half_cols(half)] for tile in (last_wgs, last_h) for half in range(2)]
+        x_second = x_second + [z_store[:, n * HALF : (n + 1) * HALF] for n in range(PACK)]
         for s in range(PACK):
             fetch(s, 1, x_second[s])
-        z_q = [quantize_z(0, woven0)]
+        z_mx = [quantize_z(0, z_words0)]
         for s in range(PACK, SLICES):
             fetch(s, 1, x_second[s])
 
-        def update_terms(half, s):
+        def y_terms_of(u):
+            half, s = divmod(u, SLICES)
             b, t = divmod(s, PACK)
-            direct = (s, half) in DIRECT2
-            ambient = ambient_tiles[half * SLICES + s]
-            z_codes, z_scales = z_q[half]
+            z_codes, z_scales = z_mx[half]
             own = slice(t * P, (t + 1) * P)
-            bank_a = take(a_banks)
+            bank = take(a_banks)
             passes = []
             for a in range(2):
-                wd_codes, wd_scales = wd_q[(a, b)]
-                passes.append((z_codes[:, half_cols(a)], z_scales[:, half_cols(a)], wd_codes[:, own].bitcast(FP8X4), wd_scales[:, own]))
-            product(bank_a, "tokens" if direct else "weights", passes)
-            return direct, (bank_a if direct else to_sbuf(bank_a, b_terms)), ambient
+                codes, scales = wd_mx[(a, b)]
+                z_pass = (z_codes[:, half_cols(a)], z_scales[:, half_cols(a)])
+                passes.append(z_pass + (codes[:, own].bitcast(FP8X4), scales[:, own]))
+            product(bank, True, passes)
+            return to_sbuf(bank, b_terms), amb_tiles[u]
 
-        def put_y(terms, half, s):
-            y = spare[:] if (half, s) == (0, 5) else take(x_ring)[:]
-            add_terms(terms, y)
-            nc.vector.tensor_tensor(
-                pages[s][:].indirect(list_half(list4, half)), y, wgo_rows[:, s % PACK, half_cols(half)], MULT
-            )
-
-        second_store = take(raw_tiles)[:].rearrange("p i c -> p (i c)").bitcast(BF16)
-        done = 0
-        terms = update_terms(0, 0)
-        for u in range(2 * SLICES):
+        def put_y(u, terms):
             half, s = divmod(u, SLICES)
-            if u == SLICES - 1:
-                put_y(terms, half, s)
-                terms = update_terms(1, 0)
-                continue
-            following = update_terms(*divmod(u + 1, SLICES)) if u + 1 < 2 * SLICES else None
-            put_y(terms, half, s)
-            terms = following
-            if half == 0:
-                for r in range(done, done + Z_AFTER[s]):
-                    make_z(r, 1, x_second[r], second_store)
-                done = done + Z_AFTER[s]
-                if s == 5:
-                    z_q.append(quantize_z(1, second_store))
-            else:
-                nc.sync.dma_start(slice_rows(out, s), pages[s][:])
+            y = spare[:] if u == QUANTISE_BEHIND else take(x_ring)[:]
+            add_transposed(terms[0], terms[1], y)
+            weights = wgo_rows[:, s % PACK, half_cols(half)]
+            nc.vector.tensor_tensor(pages[s][:].indirect(list_half(list4, half)), y, weights, MULT)
+
+        z_words1 = take(raw_tiles)[:].rearrange("p i c -> p (i c)").bitcast(BF16)
+        y_terms = {0: y_terms_of(0)}
+        made = 0
+        for u in range(UNITS):
+            if u + 1 < UNITS and u + 1 != SLICES:
+                y_terms[u + 1] = y_terms_of(u + 1)
+            put_y(u, y_terms[u])
+            if u + 1 == SLICES:
+                y_terms[u + 1] = y_terms_of(u + 1)
+            if u <= QUANTISE_BEHIND:
+                count = 2 if u < UNITS_WITH_TWO else 1
+                for s in range(made, made + count):
+                    make_z(s, 1, x_second[s], z_words1)
+                made = made + count
+            if u == QUANTISE_BEHIND:
+                z_mx.append(quantize_z(1, z_words1))
+                for later in range(AMB_IN_FIRST_STAGE, UNITS):
+                    transpose_amb(later, take(b_banks))
+            if u >= SLICES:
+                nc.sync.dma_start(slice_rows(out, u - SLICES), pages[u - SLICES][:])

from contextlib import ExitStack

import concourse.mybir as mybir
from concourse.masks import make_identity

K, H, T, S, T2 = 512, 1024, 4096, 1024, 2048
FLOPS = 2 * (2 * K * H * S + H * H * S)

F32 = mybir.dt.float32
BF16 = mybir.dt.bfloat16
I32 = mybir.dt.int32
U32 = mybir.dt.uint32
U16 = mybir.dt.uint16
U8 = mybir.dt.uint8
FP8X4 = mybir.dt.float8_e4m3fn_x4
FP4X4 = mybir.dt.float4_e2m1fn_x4
ABS = mybir.ActivationFunctionType.Abs
IDENTITY = mybir.ActivationFunctionType.Identity
MULT = mybir.AluOpType.mult
ADD = mybir.AluOpType.add

P = 128
PACK = 4
PASS = P * PACK
HALF = 512
SLICES = H // P
UNITS = 2 * SLICES
LIST_COLS = HALF // 16

TERMS_IN_STAGING = {3: 1, 7: 0, 9: 1}
AMB_FROM_SUM = UNITS - 4
AMB_BEHIND_SUMS = 8
AMB_IN_FIRST_STAGE = 12
QUANTISE_BEHIND = 5
UNITS_WITH_TWO = SLICES - (QUANTISE_BEHIND + 1)


def in_turn(tiles):
    return {"tiles": tiles, "taken": 0}


def take(turns):
    count = turns["taken"]
    turns["taken"] = count + 1
    return turns["tiles"][count % len(turns["tiles"])]


def half_cols(half):
    return slice(half * HALF, (half + 1) * HALF)


def list_half(tile, half):
    return tile[:, half * LIST_COLS : (half + 1) * LIST_COLS]


def slice_rows(matrix, s):
    b, t = divmod(s, PACK)
    return matrix[PASS * b : PASS * (b + 1), :].rearrange("(p t) c -> t p c", t=PACK)[t]


def tile_list_reefer_fault_board_kernel(
    tc, tab_words, tab_scales, w4_words, w4_scales, wa, wd, dv, amb, page0, wgs, wgo, offs, offs2, offs3, offs4, out
):
    nc = tc.nc
    with ExitStack() as ctx:
        keep = ctx.enter_context(tc.tile_pool(name="keep", bufs=1))
        psum = ctx.enter_context(tc.psum_pool(name="psum", bufs=1))

        def sbuf_in_turn(name, count, shape, dtype):
            return in_turn([keep.tile(shape, dtype, name="%s%d" % (name, n), align_bytes=64) for n in range(count)])

        def banks_in_turn(name, count):
            return in_turn([psum.tile([P, HALF], F32, name="%s%d" % (name, n)) for n in range(count)])

        raw_tiles = sbuf_in_turn("raw", 2, [P, PACK, PASS], F32)
        staging_tiles = sbuf_in_turn("staging", 2, [P, PACK * PASS], BF16)
        a_terms = sbuf_in_turn("term_a", 3, [P, HALF], F32)
        b_terms = sbuf_in_turn("term_b", 5, [P, HALF], F32)
        h_ring = sbuf_in_turn("h", 3, [P, S], F32)
        x_ring = sbuf_in_turn("x", 4, [P, HALF], F32)
        amb_tiles = [keep.tile([P, HALF], F32, name="amb%d" % u) for u in range(UNITS)]
        a_banks = banks_in_turn("bank_a", 3)
        b_banks = banks_in_turn("bank_b", 3)
        sum_banks = banks_in_turn("sum_bank", 2)
        pages = [keep.tile([P, T2], F32, name="page%d" % s) for s in range(SLICES)]

        def load_list(source, name):
            tile = keep.tile([P, S // 16], U16, name=name)
            nc.sync.dma_start(tile[:], source)
            return tile

        def load_page(s):
            nc.sync.dma_start(pages[s][:], slice_rows(page0, s))

        def load_weight_block(matrix, a, b):
            raw = take(raw_tiles)
            rows = matrix[PASS * a : PASS * (a + 1), PASS * b : PASS * (b + 1)]
            nc.sync.dma_start(raw[:], rows.rearrange("(p i) c -> p i c", i=PACK))
            return raw

        def load_on_each_quadrant(tile, rows):
            for q in range(4):
                nc.sync.dma_start(tile[32 * q : 32 * (q + 1)], rows)

        def load_amb(units):
            for u in units:
                half, s = divmod(u, SLICES)
                nc.sync.dma_start(amb_tiles[u][:], slice_rows(amb, s)[:, half_cols(half)])

        table_scales = keep.tile([P, T], U8, name="table_scales")
        nc.vector.memset(table_scales[:].bitcast(I32), 0)
        for q in range(4):
            rows = tab_scales[0, 4 * q : 4 * q + 4, :].bitcast(I32)
            nc.gpsimd.dma_start(table_scales[32 * q : 32 * q + 4, :].bitcast(I32), rows)
        identity = keep.tile([P, P], F32, name="identity")
        make_identity(nc, identity[:])

        list1 = load_list(offs, "list1")
        table_words = keep.tile([P, T], U32, name="table_words", tag="wide")
        nc.sync.dma_start(table_words[:].bitcast(I32), tab_words[0].rearrange("p c i -> p (c i)").bitcast(I32))
        w4_raw_scales = keep.tile([P, H], U8, name="w4_raw_scales")
        for q in range(4):
            rows = w4_scales[0, 4 * q : 4 * q + 4, :].bitcast(I32)
            nc.sync.dma_start(w4_raw_scales[32 * q : 32 * (q + 1), :].bitcast(I32), rows.partition_broadcast(8))
        w4_raw = keep.tile([P, 2 * H], U8, name="w4_raw")
        nc.sync.dma_start(w4_raw[:].bitcast(I32), w4_words[0].bitcast(I32))
        wa_raw0 = load_weight_block(wa, 0, 0)
        load_page(0)
        list2 = load_list(offs2, "list2")
        wgs_rows = [keep.tile([P, S], F32, name="wgs_rows%d" % t, align_bytes=64) for t in range(PACK)]
        wgs_dealt = wgs.rearrange("(q t) c -> t q c", t=PACK)
        for half in range(2):
            load_on_each_quadrant(wgs_rows[0][:, half_cols(half)], wgs_dealt[0][:, half_cols(half)])
        list3 = load_list(offs3, "list3")
        load_page(1)
        load_on_each_quadrant(wgs_rows[1][:], wgs_dealt[1])
        wa_raw1 = load_weight_block(wa, 0, 1)
        dv_rows = keep.tile([P, 2, PACK], F32, name="dv_rows")
        nc.sync.dma_start(dv_rows[:], dv.rearrange("(b p t) -> p b t", b=2, t=PACK))
        for s in range(2, PACK):
            load_page(s)
            load_on_each_quadrant(wgs_rows[s][:], wgs_dealt[s])
        wd_wide = keep.tile([P, PACK, H], F32, name="wd_wide", tag="wide")
        nc.sync.dma_start(wd_wide[:], wd[0:PASS, :].rearrange("(p i) c -> p i c", i=PACK))
        load_page(PACK)
        wd_raw = {(0, 0): wd_wide[:, :, 0:PASS], (0, 1): wd_wide[:, :, PASS:H]}

        w4_codes = keep.tile([P, 2 * H], U8, name="w4_codes", align_bytes=64)
        w4_dealt_scales = keep.tile([P, H], U8, name="w4_dealt_scales", align_bytes=64)
        nc.vector.tensor_copy(
            w4_dealt_scales[:].rearrange("p (b t m) -> p b t m", b=2, t=PACK),
            w4_raw_scales[:].rearrange("p (b m t) -> p b t m", b=2, t=PACK),
        )
        nc.vector.tensor_copy(
            w4_codes[:].bitcast(U16).rearrange("p (b t m) -> p b t m", b=2, t=PACK),
            w4_raw[:].bitcast(U16).rearrange("p (b m t) -> p b t m", b=2, t=PACK),
        )

        def cast_columns(staging, raw, first, count):
            part = staging[:, first * PASS : (first + count) * PASS]
            dealt = raw.rearrange("p i (m t) -> p m t i", t=PACK)[:, :, first : first + count, :]
            nc.scalar.copy(part.rearrange("p (t m i) -> p m t i", t=count, i=PACK), dealt)
            return part

        def cast_weight_block(raw):
            return cast_columns(take(staging_tiles), raw, 0, PACK)

        def quantize_weight_block(staged, codes, name):
            scales = keep.tile([P, PASS], U8, name=name + "_scales", align_bytes=64)
            nc.vector.quantize_mx(codes.bitcast(FP8X4), scales[:], staged)
            return codes, scales

        wa0_codes = keep.tile([P, PASS], U32, name="wa0_codes", align_bytes=64)
        wa0_scales = keep.tile([P, PASS], U8, name="wa0_scales", align_bytes=64)
        wa0_staging = take(staging_tiles)
        for first, count in ((0, 1), (1, PACK - 1)):
            part = cast_columns(wa0_staging, wa_raw0[:], first, count)
            cols = slice(first * P, (first + count) * P)
            nc.vector.quantize_mx(wa0_codes[:, cols].bitcast(FP8X4), wa0_scales[:, cols], part)
        wa_mx = [(wa0_codes[:], wa0_scales)]

        picked = []
        for half in range(2):
            words = keep.tile([P, HALF], U32, name="picked_words%d" % half, align_bytes=64)
            scales = keep.tile([P, HALF], U8, name="picked_scales%d" % half, align_bytes=64)
            nc.vector.tensor_copy(words[:], table_words[:].indirect(list_half(list1, half)))
            nc.vector.tensor_copy(scales[:], table_scales[:].indirect(list_half(list1, half)))
            picked.append((words, scales))

        def product(bank, transposed, passes):
            last = len(passes) - 1
            if not transposed:
                for a, (codes, scales, w_codes, w_scales) in enumerate(passes):
                    nc.tensor.matmul_mx(
                        bank[:], w_codes, w_scales, codes.bitcast(FP8X4), scales, start=(a == 0), stop=(a == last)
                    )
                return
            for j in range(HALF // P):
                cols = slice(j * P, (j + 1) * P)
                for a, (codes, scales, w_codes, w_scales) in enumerate(passes):
                    nc.tensor.matmul_mx(
                        bank[:, cols], codes[:, cols].bitcast(FP8X4), scales[:, cols], w_codes, w_scales,
                        start=(a == 0), stop=(a == last),
                    )

        def to_sbuf(bank, terms):
            term = take(terms)
            nc.scalar.copy(term[:], bank[:])
            return term

        def add_transposed(first, second, result):
            bank = take(sum_banks)
            for j in range(HALF // P):
                cols = slice(j * P, (j + 1) * P)
                nc.tensor.matmul(bank[:, cols], first[:, cols], identity[:], start=True, stop=False, is_transpose=True)
                nc.tensor.matmul(bank[:, cols], second[:, cols], identity[:], start=False, stop=True, is_transpose=True)
            nc.scalar.copy(result, bank[:])

        def h_terms_of(u):
            s, half = divmod(u, 2)
            b, t = divmod(s, PACK)
            words, scales = picked[half]
            wa_codes, wa_scales = wa_mx[b]
            own = slice(t * P, (t + 1) * P)
            bank_a = take(a_banks)
            bank_b = take(b_banks)
            w4_own = w4_codes[:, 2 * s * P : 2 * (s + 1) * P].bitcast(FP4X4)
            product(bank_b, s > 0, [(words[:], scales[:], w4_own, w4_dealt_scales[:, s * P : (s + 1) * P])])
            product(bank_a, s > 0, [(words[:], scales[:], wa_codes[:, own].bitcast(FP8X4), wa_scales[:, own])])
            if u in TERMS_IN_STAGING:
                staged = staging_tiles["tiles"][TERMS_IN_STAGING[u]][:].bitcast(F32)
                nc.scalar.activation(staged[:, 0:HALF], bank_b[:], ABS)
                nc.scalar.copy(staged[:, HALF:S], bank_a[:])
                return staged[:, HALF:S], staged[:, 0:HALF]
            term_b = b_terms["tiles"][2 * half + s % 2]
            nc.scalar.activation(term_b[:], bank_b[:], ABS)
            return (to_sbuf(bank_a, a_terms) if s > 0 else bank_a), term_b

        h_tiles = {}
        h_single = keep.tile([P, S], F32, name="h_single", align_bytes=64)
        h_terms = {}

        def h_step(u):
            if u + 1 < UNITS:
                h_terms[u + 1] = h_terms_of(u + 1)
            s, half = divmod(u, 2)
            if half == 0:
                h_tiles[s] = h_single if s == 1 else take(h_ring)
            term_a, term_b = h_terms[u]
            if s == 0:
                nc.vector.tensor_tensor(h_tiles[s][:, half_cols(half)], term_a[:], term_b[:], ADD)
            else:
                add_transposed(term_a, term_b, h_tiles[s][:, half_cols(half)])

        def put_h(s, offsets, cols):
            h, weights = h_tiles[s][:, cols], wgs_rows[s % PACK][:, cols]
            nc.vector.tensor_tensor(pages[s][:].indirect(offsets), h, weights, MULT)

        def fetch(s, half, x):
            nc.vector.tensor_copy(x, pages[s][:].indirect(list_half(list3, half)))

        z_rows = keep.tile([P, PACK, HALF], BF16, name="z_rows")

        def make_z(s, half, x, z_words):
            b, t = divmod(s, PACK)
            magnitude = b_terms["tiles"][(s + 1) % 2] if half == 0 else take(b_terms)
            nc.scalar.activation(magnitude[:], x, ABS)
            nc.scalar.activation(z_rows[:, t, :], magnitude[:], IDENTITY, bias=dv_rows[:, b, t : t + 1])
            if t == PACK - 1:
                target = z_words[:, b * PACK * HALF : (b + 1) * PACK * HALF]
                nc.scalar.copy(
                    target.rearrange("p (c i t) -> p c t i", i=4, t=PACK),
                    z_rows[:].rearrange("p t (c i) -> p c t i", i=4),
                )

        def quantize_z(half, z_words):
            codes = keep.tile([P, 2 * HALF], U32, name="z_codes%d" % half, tag="z_codes%d" % half, align_bytes=64)
            scales = keep.tile([P, 2 * HALF], U8, name="z_scales%d" % half, align_bytes=64)
            nc.vector.quantize_mx(codes[:].bitcast(FP8X4), scales[:], z_words)
            return codes, scales

        def transpose_amb(u, bank):
            for j in range(HALF // P):
                cols = slice(j * P, (j + 1) * P)
                nc.tensor.transpose(bank[:, cols], amb_tiles[u][:, cols], identity[:])
            nc.scalar.copy(amb_tiles[u][:], bank[:])

        z_store = keep.tile([P, PACK * HALF], F32, name="z_store", align_bytes=64)
        z_words0 = z_store[:].bitcast(BF16)
        h_terms[0] = h_terms_of(0)
        ahead = 5
        for u in range(ahead):
            h_step(u)
            if u < 2:
                put_h(0, list_half(list2, u), half_cols(u))
        wa1_staged = cast_weight_block(wa_raw1[:])

        load_amb(range(0, AMB_BEHIND_SUMS // 2))
        wd_raw[(1, 0)] = load_weight_block(wd, 1, 0)[:]
        load_amb(range(AMB_BEHIND_SUMS // 2, AMB_BEHIND_SUMS))
        load_page(5)
        wd_raw[(1, 1)] = load_weight_block(wd, 1, 1)[:]
        load_page(6)
        load_amb(range(AMB_BEHIND_SUMS, UNITS))
        load_page(7)
        list4 = load_list(offs4, "list4")

        spare = keep.tile([P, HALF], F32, name="spare", tag="z_codes1", align_bytes=64)
        x_first = {}
        wd_staged = {}
        wd_mx = {}
        for s in range(SLICES):
            if s > 0:
                put_h(s, list2[:], slice(0, S))
            x_first[s] = spare if s == SLICES - 1 else take(x_ring)
            fetch(s, 0, x_first[s][:])
            if s == 1:
                wa1_codes = keep.tile([P, PASS], U32, name="wa1_codes", tag="h_single", align_bytes=64)
                wa_mx.append(quantize_weight_block(wa1_staged, wa1_codes[:], "wa1"))
            if s in (PACK, PACK + 2):
                a = (s - PACK) // 2
                wd_codes = keep.tile([P, H], U32, name="wd_codes%d" % a, tag="wgs_rows%d" % (s - PACK), align_bytes=64)
                for b in range(2):
                    codes = wd_codes[:, half_cols(b)]
                    wd_mx[(a, b)] = quantize_weight_block(wd_staged[(a, b)], codes, "wd%d%d" % (a, b))
            for u in range(ahead + 2 * s, min(ahead + 2 * s + 2, UNITS)):
                h_step(u)
                if u >= AMB_FROM_SUM:
                    for n in range(2 * (u - AMB_FROM_SUM), 2 * (u - AMB_FROM_SUM) + 2):
                        transpose_amb(n, take(sum_banks))
            if s >= 1:
                make_z(s - 1, 0, x_first[s - 1][:], z_words0)
            if 2 <= s < 6:
                wd_staged[divmod(s - 2, 2)] = cast_weight_block(wd_raw[divmod(s - 2, 2)])
            if s == 3:
                wgo_rows = keep.tile([P, PACK, S], F32, name="wgo_rows", tag="wide")
                load_on_each_quadrant(wgo_rows[:], wgo.rearrange("(q t) c -> q t c", t=PACK))
            if s == 5:
                for u in range(AMB_BEHIND_SUMS, AMB_IN_FIRST_STAGE):
                    transpose_amb(u, take(b_banks if u % 2 == 0 else a_banks))
        make_z(SLICES - 1, 0, x_first[SLICES - 1][:], z_words0)

        last_wgs, last_h = wgs_rows[PACK - 1], h_tiles[SLICES - 1]
        x_second = [tile[:, half_cols(half)] for tile in (last_wgs, last_h) for half in range(2)]
        x_second = x_second + [z_store[:, n * HALF : (n + 1) * HALF] for n in range(PACK)]
        for s in range(PACK):
            fetch(s, 1, x_second[s])
        z_mx = [quantize_z(0, z_words0)]
        for s in range(PACK, SLICES):
            fetch(s, 1, x_second[s])

        def y_terms_of(u):
            half, s = divmod(u, SLICES)
            b, t = divmod(s, PACK)
            z_codes, z_scales = z_mx[half]
            own = slice(t * P, (t + 1) * P)
            bank = take(a_banks)
            passes = []
            for a in range(2):
                codes, scales = wd_mx[(a, b)]
                z_pass = (z_codes[:, half_cols(a)], z_scales[:, half_cols(a)])
                passes.append(z_pass + (codes[:, own].bitcast(FP8X4), scales[:, own]))
            product(bank, True, passes)
            return to_sbuf(bank, b_terms), amb_tiles[u]

        def put_y(u, terms):
            half, s = divmod(u, SLICES)
            y = spare[:] if u == QUANTISE_BEHIND else take(x_ring)[:]
            add_transposed(terms[0], terms[1], y)
            weights = wgo_rows[:, s % PACK, half_cols(half)]
            nc.vector.tensor_tensor(pages[s][:].indirect(list_half(list4, half)), y, weights, MULT)

        z_words1 = take(raw_tiles)[:].rearrange("p i c -> p (i c)").bitcast(BF16)
        y_terms = {0: y_terms_of(0)}
        made = 0
        for u in range(UNITS):
            if u + 1 < UNITS and u + 1 != SLICES:
                y_terms[u + 1] = y_terms_of(u + 1)
            put_y(u, y_terms[u])
            if u + 1 == SLICES:
                y_terms[u + 1] = y_terms_of(u + 1)
            if u <= QUANTISE_BEHIND:
                count = 2 if u < UNITS_WITH_TWO else 1
                for s in range(made, made + count):
                    make_z(s, 1, x_second[s], z_words1)
                made = made + count
            if u == QUANTISE_BEHIND:
                z_mx.append(quantize_z(1, z_words1))
                for later in range(AMB_IN_FIRST_STAGE, UNITS):
                    transpose_amb(later, take(b_banks))
            if u >= SLICES:
                nc.sync.dma_start(slice_rows(out, u - SLICES), pages[u - SLICES][:])
